import numpy as np
import ml_dtypes


def mxq(x, axis, fmt="e4m3"):
    dtype, down = {"e4m3": (ml_dtypes.float8_e4m3fn, 7), "e5m2": (ml_dtypes.float8_e5m2, 14)}[fmt]
    v = np.moveaxis(np.asarray(x, np.float32).astype(ml_dtypes.bfloat16).astype(np.float64), axis, -1)
    blocks = v.reshape(v.shape[:-1] + (-1, 32))
    amax = np.abs(blocks).max(-1, keepdims=True)
    byte = np.maximum(np.where(amax > 0, np.frexp(amax)[1] - 1 + 127, 0) - down, 1)
    scale = np.exp2(byte - 127.0)
    codes = (blocks / scale).astype(np.float32).astype(dtype).astype(np.float64)
    return np.moveaxis((codes * scale).reshape(v.shape), -1, axis)


WIDE = False


def mx_kscale(k):
    if not WIDE:
        return np.ones(k)
    levels = np.array([10, -10, 5, -5, 0])
    if k % 512:
        return np.exp2(np.random.permutation(np.resize(levels, k // 32))).repeat(32)
    a = np.empty((k // 512, 16))
    for p in range(k // 512):
        a[p, :8] = np.random.permutation(np.resize(levels, 8))
        for g in range(8):
            far = levels[np.abs(levels - a[p, g]) >= 10]
            a[p, g + 8] = far[np.random.randint(len(far))]
    return np.exp2(a.ravel()).repeat(32)


BF16 = ml_dtypes.bfloat16


def bf(x):
    return np.asarray(x, np.float32).astype(BF16)


def f64(x):
    return np.asarray(x).astype(np.float64)


E2M1 = np.array([0.0, 0.5, 1.0, 1.5, 2.0, 3.0, 4.0, 6.0, -0.0, -0.5, -1.0, -1.5, -2.0, -3.0, -4.0, -6.0])


def pack_weight(w, fmt):
    k, n = w.shape
    w = f64(bf(w)).reshape(k // 32, 32, n)
    amax = np.abs(w).max(1)
    if fmt == "e4m3":
        byte = np.frexp(amax)[1] - 1 + 127 - 7
    else:
        mant, ex = np.frexp(amax / 6.0)
        byte = np.where(mant > 0.5, ex, ex - 1) + 127
    byte = np.clip(np.where(amax > 0, byte, 1), 1, 254)
    scaled = (w * np.exp2(127.0 - byte)[:, None, :]).reshape(k, n).astype(np.float32)
    by_word = np.ascontiguousarray(scaled.reshape(k // 512, 128, 4, n).transpose(0, 1, 3, 2))
    if fmt == "e4m3":
        words = by_word.astype(ml_dtypes.float8_e4m3fn).view(np.uint8)
    else:
        c = by_word.astype(ml_dtypes.float4_e2m1fn).view(np.uint8) & 0xF
        words = c[..., 0::2] | (c[..., 1::2] << 4)
    return np.ascontiguousarray(words), np.ascontiguousarray(byte.astype(np.uint8).reshape(k // 512, 16, n))


def unpack_weight(words, scales, fmt):
    g, p, n, _ = words.shape
    if fmt == "e4m3":
        vals = np.ascontiguousarray(words).view(ml_dtypes.float8_e4m3fn).astype(np.float64)
    else:
        nib = np.empty((g, p, n, 4), np.uint8)
        nib[..., 0::2] = words & 0xF
        nib[..., 1::2] = words >> 4
        vals = E2M1[nib]
    vals = vals * np.repeat(np.exp2(scales.astype(np.float64) - 127.0), 8, axis=1)[..., None]
    return vals.transpose(0, 1, 3, 2).reshape(g * 512, n)
def pack4(w):
    words, scales = pack_weight(w, "e2m1")
    return words.reshape(words.shape[0], 128, -1), scales


def unpack4(words, scales):
    return unpack_weight(words.reshape(words.shape[0], 128, -1, 2), scales, "e2m1")


def planes(Y):
    n, m = Y.shape
    b = f64(bf(Y)).reshape(n // 32, 32, m)
    amax = np.abs(b).max(1)
    byte = np.clip(np.where(amax > 0, np.frexp(amax)[1] - 1 + 127 - 7, 1), 1, 254)
    codes = (b * np.exp2(127.0 - byte)[:, None, :]).reshape(n, m).astype(np.float32).astype(ml_dtypes.float8_e4m3fn).view(np.uint8)
    words = codes.reshape(n // 512, 128, 4, m).transpose(0, 1, 3, 2)
    return np.ascontiguousarray(words), np.ascontiguousarray(byte.astype(np.uint8).reshape(n // 512, 16, m))


B, F, R, C, RI, NL, FL, TT, KN, KF, KL, P = 128, 16, 4, 32, 2, 2, 4, 4, 512, 1024, 1024, 1024

def neighbours(d, lines):
    pts = [np.roll(d, (-i, -j), (0, 1)) for i in lines for j in range(TT)]
    return np.concatenate(pts, axis=2).reshape(B * F, -1)

def real_form(z):
    return np.block([[z.real, -z.imag], [z.imag, z.real]])

def setup_inputs():
    sn, sf, t = mx_kscale(KN), mx_kscale(KF), mx_kscale(KL)
    d = np.random.randn(B, F, C) + 1j * np.random.randn(B, F, C)
    near = real_form(neighbours(d, range(NL)))
    far = real_form(neighbours(d, list(range(-FL // 2, 0)) + list(range(NL, NL + FL // 2))))
    w_near = 0.8 * np.random.randn(KN, R * C) / np.sqrt(KN)
    w_far = 0.5 * np.random.randn(KF, R * C) / np.sqrt(KF)
    w_far_words, w_far_scales = pack4(w_far / sf[:, None])
    line_gain = 0.5 + np.random.rand(KL)
    shade = 0.5 * np.exp(0.6 * np.random.randn(P))
    line = R * np.arange(B)[None, :] + np.arange(R)[:, None]
    a = 2 * np.pi * (np.arange(P) + 0.5)[:, None, None] * line[None] / P
    re = np.stack([np.cos(a), -np.sin(a)], axis=2).reshape(P, KL)
    im = np.stack([np.sin(a), np.cos(a)], axis=2).reshape(P, KL)
    op = np.concatenate([shade[:, None] * re, shade[:, None] * im], axis=0) / np.sqrt(R * B)
    rest = shade[:, None, None] ** 2 * (np.random.randn(P, F, C) ** 2 + np.random.randn(P, F, C) ** 2)
    return {"near": bf(near * sn), "far": bf(far * sf), "w_near": bf(w_near / sn[:, None]),
            "w_far_words": w_far_words, "w_far_scales": w_far_scales,
            "line_gain": bf(line_gain * t), "image_op": bf(op / t), "rest": bf(rest)}

def reference(near, far, w_near, w_far_words, w_far_scales, line_gain, image_op, rest):
    k_near = mxq(f64(near), 1) @ mxq(f64(w_near), 0)
    k_far = mxq(f64(far), 1) @ unpack4(w_far_words, w_far_scales)
    h = (k_near + k_far).reshape(RI * B, F, R, C).transpose(2, 0, 1, 3).reshape(KL, F * C)
    h = h * f64(line_gain)[:, None]
    img = (mxq(f64(image_op), 1) @ mxq(h, 0)).reshape(RI, P, F, C)
    sq = img * img
    y = np.sqrt(sq[0] + sq[1] + f64(rest))
    Y = y.reshape(P, F * C)
    words, scales = planes(Y)
    return y, words, scales

@@ -1,0 +1,362 @@
+from contextlib import ExitStack
+
+import concourse.mybir as mybir
+from concourse.masks import make_identity
+
+F32 = mybir.dt.float32
+BF16 = mybir.dt.bfloat16
+I32 = mybir.dt.int32
+U32 = mybir.dt.uint32
+U8 = mybir.dt.uint8
+FP8X4 = mybir.dt.float8_e4m3fn_x4
+FP4X4 = mybir.dt.float4_e2m1fn_x4
+ACT = mybir.ActivationFunctionType
+ALU = mybir.AluOpType
+
+FLOPS = 2 * 4096 * 1536 * 128 + 2 * 2048 * 1024 * 512
+
+P = 128
+PAIRS = 8
+TILES = 8
+LOADS_AHEAD = 5
+
+
+def tile_grappa_coil_group_rss_k6_kernel(
+    tc, near, far, w_near, w_far_words, w_far_scales, line_gain, image_op, rest, out_0, out_1, out_2
+):
+    nc = tc.nc
+    near_v = near.rearrange("(p e f) k -> p e (f k)", p=P, e=2)
+    far_v = far.rearrange("(p e f) k -> p e (f k)", p=P, e=2)
+    op_v = image_op.rearrange("(a g p t) k -> g p a (t k)", a=2, g=2, t=4)
+    rest_v = rest.rearrange("(g p t) f c -> g p t (f c)", g=2, t=4)
+    y_v = out_0.rearrange("(g p t) f c -> g p t (f c)", g=2, t=4)
+    gain_v = line_gain.rearrange("(r q t) -> q r t", r=4, t=4)
+
+    with ExitStack() as ctx:
+        keep = ctx.enter_context(tc.tile_pool(name="keep", bufs=1))
+        ring = ctx.enter_context(tc.tile_pool(name="ring", bufs=1))
+        psum = ctx.enter_context(tc.psum_pool(name="psum", bufs=1))
+        ctx.enter_context(tc.manual_schedule())
+
+        ident = keep.tile([P, P], F32, name="ident")
+        wn_raw = keep.tile([P, 4, 128], BF16, name="wn_raw")
+        wn_grp = keep.tile([P, 128, 4], BF16, name="wn_grp", align_bytes=64)
+        wn_codes = keep.tile([P, 128], U32, name="wn_codes", align_bytes=64)
+        wn_scales = keep.tile([P, 128], U8, name="wn_scales", align_bytes=64)
+        wf_words = keep.tile([P, 512], U8, name="wf_words", align_bytes=64)
+        wf_scales = keep.tile([P, 256], U8, name="wf_scales", align_bytes=64)
+        gain = keep.tile([P, 4, 4], BF16, name="gain")
+        warm = keep.tile([P, 1], F32, name="warm")
+        h_tmp = keep.tile([P, 4, PAIRS * 128], BF16, name="h_tmp", align_bytes=64)
+        h_fin = keep.tile([P, 2, 2, PAIRS * 128], BF16, name="h_fin", align_bytes=64)
+        h_codes = keep.tile([P, 2, 512], U32, name="h_codes", align_bytes=64)
+        h_scales = keep.tile([P, 2, 512], U8, name="h_scales", align_bytes=64)
+        y_scales = keep.tile([P, 2, 512], U8, name="y_scales", align_bytes=64)
+
+        near_raw, far_raw, far_sorted, op_raw, rest_sb = {}, {}, {}, {}, {}
+        grouped, codes, scales, acc, banks = {}, {}, {}, {}, {}
+        sq_re, sq_im, y_sb, y_bf, y_codes = {}, {}, {}, {}, {}
+
+        def bank(b):
+            return psum.tile([P, 512], F32, name="bank%d" % b)
+
+        def load_pair(j):
+            near_raw[j] = ring.tile([P, 2, 1024], BF16, name="near_raw", bufs=LOADS_AHEAD)
+            nc.sync.dma_start(out=near_raw[j][:], in_=near_v[:, :, 1024 * j : 1024 * (j + 1)])
+            for e in range(2):
+                far_raw[j, e] = ring.tile([P, 2048], BF16, name="far_raw", bufs=2 * LOADS_AHEAD)
+                nc.sync.dma_start(out=far_raw[j, e][:], in_=far_v[:, e, 2048 * j : 2048 * (j + 1)])
+
+        def load_op(n):
+            op_raw[n] = keep.tile([P, 2, 2048], BF16, name="op_raw%d" % n)
+            nc.sync.dma_start(out=op_raw[n][:], in_=op_v[n // 2][:, :, 2048 * (n % 2) : 2048 * (n % 2 + 1)])
+
+        def load_rest(g):
+            rest_sb[g] = keep.tile([P, 4, 512], BF16, name="rest%d" % g)
+            nc.sync.dma_start(out=rest_sb[g][:], in_=rest_v[g])
+
+        def sort_far(j, e):
+            far_sorted[j, e] = ring.tile([P, 1024], F32, name="far_sorted", bufs=4)
+            nc.vector.tensor_copy(
+                out=far_sorted[j, e][:].rearrange("p (s u j i) -> p s j u i", s=4, u=2, i=4),
+                in_=far_raw[j, e][:].bitcast(F32).rearrange("p (s j i u) -> p s j u i", s=4, u=2, i=4),
+            )
+
+        def new_group(key):
+            grouped[key] = ring.tile([P, 2048], BF16, name="grouped", bufs=4, align_bytes=64)
+
+        def quantize(key):
+            codes[key] = ring.tile([P, 512], U32, name="codes", bufs=7, align_bytes=64)
+            scales[key] = ring.tile([P, 512], U8, name="scales", bufs=7, align_bytes=64)
+            nc.vector.quantize_mx(out=codes[key][:].bitcast(FP8X4), scales=scales[key][:], in_=grouped[key][:])
+
+        def turn_pair(j, q):
+            new_group((j, q))
+            for s in range(2):
+                bk = bank(2 * q + s)
+                for h in range(2):
+                    for u in range(2):
+                        if q == 0:
+                            words = near_raw[j][:].rearrange("p e x -> p (e x)").bitcast(F32)
+                            base = 512 * s + 256 * h
+                            src = words[:, base + u : base + 256 : 2]
+                        else:
+                            base = ((2 * h + s) * 2 + u) * 128
+                            src = far_sorted[j, q - 1][:, base : base + 128]
+                        nc.tensor.transpose(bk[:, (2 * h + u) * 128 : (2 * h + u + 1) * 128], src, ident[:])
+                nc.scalar.copy(
+                    out=grouped[j, q][:, 1024 * s : 1024 * (s + 1)].bitcast(F32).rearrange(
+                        "p (v h m u) -> p v h m u", v=2, h=2, u=2
+                    ),
+                    in_=bk[:].rearrange("p (h u m v) -> p v h m u", h=2, u=2, v=2),
+                )
+
+        def multiply_pair(j):
+            acc[j] = bank(6 + j % 2)
+            for e in range(2):
+                for v in range(2):
+                    t = 2 * v + e
+                    out = acc[j][:, 128 * t : 128 * (t + 1)]
+                    c0 = 256 * e + 128 * v
+                    nc.tensor.matmul_mx(
+                        out=out,
+                        lhsT=codes[j, 0][:, c0 : c0 + 128].bitcast(FP8X4),
+                        lhsT_scale=scales[j, 0][:, c0 : c0 + 128],
+                        rhs=wn_codes[:].bitcast(FP8X4),
+                        rhs_scale=wn_scales[:],
+                        start=True,
+                        stop=False,
+                    )
+                    for g in range(2):
+                        c0 = 256 * g + 128 * v
+                        nc.tensor.matmul_mx(
+                            out=out,
+                            lhsT=codes[j, 1 + e][:, c0 : c0 + 128].bitcast(FP8X4),
+                            lhsT_scale=scales[j, 1 + e][:, c0 : c0 + 128],
+                            rhs=wf_words[:, 256 * g : 256 * (g + 1)].bitcast(FP4X4),
+                            rhs_scale=wf_scales[:, 128 * g : 128 * (g + 1)],
+                            start=False,
+                            stop=(g == 1),
+                        )
+
+        def gain_pair(j):
+            nc.vector.tensor_tensor(
+                out=h_tmp[:, :, 128 * j : 128 * (j + 1)].rearrange("p r (c t) -> p r c t", t=4),
+                in0=acc[j][:].rearrange("p (t r c) -> p r c t", t=4, r=4),
+                in1=gain[:].unsqueeze(2).to_broadcast([P, 4, 32, 4]),
+                op=ALU.mult,
+            )
+
+        def swap(j0, j1):
+            cols = slice(128 * j0, 128 * j1)
+            for h in range(2):
+                for r in range(2):
+                    nc.sync.dma_start(
+                        out=h_fin[64 * r : 64 * (r + 1), :, h, cols],
+                        in_=h_tmp[64 * h : 64 * (h + 1), r::2, cols],
+                    )
+
+        def quantize_h(j0, j1):
+            for g in range(2):
+                for h in range(2):
+                    out_cols = slice(256 * h + 32 * j0, 256 * h + 32 * j1)
+                    nc.vector.quantize_mx(
+                        out=h_codes[:, g, out_cols].bitcast(FP8X4),
+                        scales=h_scales[:, g, out_cols],
+                        in_=h_fin[:, g, h, 128 * j0 : 128 * j1],
+                    )
+
+        def turn_op(i):
+            new_group(("op", i))
+            words = op_raw[i // 2][:].rearrange("p a x -> p (a x)").bitcast(F32)
+            for a in range(2):
+                bk = bank(2 * (i % 2) + a)
+                banks[i, a] = bk
+                for g in range(2):
+                    for u in range(2):
+                        base = 1024 * a + 512 * (i % 2) + 256 * g
+                        nc.tensor.transpose(
+                            bk[:, (2 * g + u) * 128 : (2 * g + u + 1) * 128],
+                            words[:, base + u : base + 256 : 2],
+                            ident[:],
+                        )
+
+        def copy_op(i, a, on_scalar):
+            out = grouped["op", i][:, 1024 * a : 1024 * (a + 1)].bitcast(F32).rearrange("p (g m u) -> p g m u", g=2, u=2)
+            src = banks[i, a][:].rearrange("p (g u m) -> p g m u", g=2, u=2)
+            if on_scalar:
+                nc.scalar.copy(out=out, in_=src)
+            else:
+                nc.vector.tensor_copy(out=out, in_=src)
+
+        def multiply_op(i):
+            for a in range(2):
+                acc["op", i, a] = bank(4 + 2 * (i % 2) + a)
+                for g in range(2):
+                    c0 = 256 * a + 128 * g
+                    nc.tensor.matmul_mx(
+                        out=acc["op", i, a][:],
+                        lhsT=codes["op", i][:, c0 : c0 + 128].bitcast(FP8X4),
+                        lhsT_scale=scales["op", i][:, c0 : c0 + 128],
+                        rhs=h_codes[:, g, :].bitcast(FP8X4),
+                        rhs_scale=h_scales[:, g, :],
+                        start=(g == 0),
+                        stop=(g == 1),
+                    )
+
+        def square(i):
+            sq_re[i] = ring.tile([P, 512], F32, name="sq_re", bufs=3)
+            sq_im[i] = ring.tile([P, 512], F32, name="sq_im", bufs=3)
+            for a, sq in enumerate((sq_re[i], sq_im[i])):
+                nc.scalar.activation(
+                    out=sq[:].rearrange("p (j h c) -> p j h c", h=2, c=32),
+                    in_=acc["op", i, a][:].rearrange("p (h j c) -> p j h c", h=2, c=32),
+                    func=ACT.Square,
+                )
+
+        def add_rest(i):
+            nc.vector.tensor_tensor(out=sq_re[i][:], in0=sq_re[i][:], in1=rest_sb[i // 4][:, i % 4, :], op=ALU.add)
+
+        def add_im(i, cols=slice(0, 512)):
+            nc.vector.tensor_tensor(out=sq_re[i][:, cols], in0=sq_re[i][:, cols], in1=sq_im[i][:, cols], op=ALU.add)
+
+        def root(i, cols=slice(0, 512)):
+            g, t = divmod(i, 4)
+            nc.scalar.activation(out=y_sb[g][:, t, cols], in_=sq_re[i][:, cols], func=ACT.Sqrt)
+            nc.sync.dma_start(out=y_v[g][:, t, cols], in_=y_sb[g][:, t, cols])
+
+        def round_y(g, cols=slice(0, 512)):
+            nc.vector.tensor_copy(
+                out=y_bf[g][:, cols, :].rearrange("p (c i) t -> p c t i", i=4),
+                in_=y_sb[g][:, :, cols].rearrange("p t (c i) -> p c t i", i=4),
+            )
+
+        def quantize_y(g, cols=slice(0, 512)):
+            nc.vector.quantize_mx(
+                out=y_codes[g][:, cols].bitcast(FP8X4),
+                scales=y_scales[:, g, cols],
+                in_=y_bf[g][:, cols, :].rearrange("p m t -> p (m t)"),
+            )
+            nc.sync.dma_start(
+                out=out_1[g][:, cols, :].rearrange("p m t -> p (m t)").bitcast(I32), in_=y_codes[g][:, cols].bitcast(I32)
+            )
+
+        for g in range(2):
+            y_sb[g] = keep.tile([P, 4, 512], F32, name="y%d" % g)
+            y_bf[g] = keep.tile([P, 512, 4], BF16, name="y_bf%d" % g, align_bytes=64)
+            y_codes[g] = keep.tile([P, 512], U32, name="y_codes%d" % g, align_bytes=64)
+
+        nc.vector.memset(wf_scales[:].bitcast(I32), 0)
+        nc.vector.memset(warm[:], 1.0)
+        make_identity(nc, ident[:])
+        for q in range(4):
+            nc.scalar.dma_start(
+                out=wf_scales[32 * q : 32 * q + 4, :].bitcast(I32).rearrange("p (g n) -> p g n", g=2),
+                in_=w_far_scales[:, 4 * q : 4 * q + 4, :].bitcast(I32).rearrange("g r n -> r g n"),
+            )
+        for h in range(2):
+            nc.scalar.dma_start(out=gain[64 * h : 64 * (h + 1)], in_=gain_v)
+        nc.scalar.activation(out=warm[:], in_=warm[:], func=ACT.Sqrt)
+        load_pair(0)
+        nc.sync.dma_start(out=wn_raw[:], in_=w_near.rearrange("(p j) n -> p j n", j=4))
+        nc.sync.dma_start(
+            out=wf_words[:].bitcast(I32).rearrange("p (g n) -> p g n", g=2),
+            in_=w_far_words.bitcast(I32).rearrange("g p n -> p g n"),
+        )
+        for j in range(1, LOADS_AHEAD):
+            load_pair(j)
+        sort_far(0, 0)
+        sort_far(0, 1)
+        nc.vector.tensor_copy(out=wn_grp[:], in_=wn_raw[:].rearrange("p j n -> p n j"))
+
+        for j in range(PAIRS):
+            if j >= 2:
+                gain_pair(j - 2)
+            if j >= 1:
+                quantize((j - 1, 2))
+            if j + 1 < PAIRS:
+                sort_far(j + 1, 0)
+            if j == 0:
+                nc.vector.quantize_mx(
+                    out=wn_codes[:].bitcast(FP8X4), scales=wn_scales[:], in_=wn_grp[:].rearrange("p n j -> p (n j)")
+                )
+            for q in range(3):
+                turn_pair(j, q)
+            quantize((j, 0))
+            if j + 1 < PAIRS:
+                sort_far(j + 1, 1)
+            elif j + 1 == PAIRS:
+                quantize_h(0, 4)
+            quantize((j, 1))
+            if j >= 1:
+                multiply_pair(j - 1)
+            if j + LOADS_AHEAD < PAIRS:
+                load_pair(j + LOADS_AHEAD)
+            if j == 3:
+                load_op(0)
+            if j == 5:
+                swap(0, 4)
+                load_op(1)
+                load_rest(0)
+
+        gain_pair(PAIRS - 2)
+        quantize((PAIRS - 1, 2))
+        turn_op(0)
+        multiply_pair(PAIRS - 1)
+        gain_pair(PAIRS - 1)
+        swap(4, 8)
+        load_op(2)
+        load_op(3)
+        load_rest(1)
+        for i in range(4):
+            if i > 0:
+                turn_op(i)
+            copy_op(i, 0, True)
+            copy_op(i, 1, True)
+            if i < 3:
+                quantize(("op", i))
+        quantize_h(4, 8)
+        quantize(("op", 3))
+
+        for i in range(0, TILES, 2):
+            ahead = i + 4 < TILES
+            multiply_op(i)
+            multiply_op(i + 1)
+            if ahead:
+                turn_op(i + 4)
+                turn_op(i + 5)
+            square(i)
+            if i == 6:
+                root(i - 1)
+            add_rest(i)
+            if i == 4:
+                round_y(0)
+            add_im(i)
+            square(i + 1)
+            add_rest(i + 1)
+            if i == 4:
+                quantize_y(0)
+            if i + 2 < TILES:
+                add_im(i + 1)
+            root(i)
+            if ahead:
+                copy_op(i + 4, 0, True)
+                root(i + 1)
+                copy_op(i + 5, 0, True)
+                copy_op(i + 4, 1, False)
+                copy_op(i + 5, 1, False)
+                quantize(("op", i + 4))
+                quantize(("op", i + 5))
+        halves = (slice(0, 256), slice(256, 512))
+        for cols in halves:
+            add_im(TILES - 1, cols)
+            root(TILES - 1, cols)
+        for cols in halves:
+            round_y(1, cols)
+        for cols in halves:
+            quantize_y(1, cols)
+        for q in range(4):
+            nc.scalar.dma_start(
+                out=out_2[:, 4 * q : 4 * q + 4, :].bitcast(I32).rearrange("g r m -> r g m"),
+                in_=y_scales[32 * q : 32 * q + 4].bitcast(I32),
+            )

@@ -18,7 +18,16 @@ FLOPS = 2 * 4096 * 1536 * 128 + 2 * 2048 * 1024 * 512
 P = 128
 PAIRS = 8
 TILES = 8
-LOADS_AHEAD = 5
+FAR_BUFS = 5
+SORTED = (0, 1)
+NEAR_N = 1
+CODE_BUFS = 7
+QH = 5
+LA = 2
+LR = 3
+R0 = 13
+V_COPY = (2, 3, 4, 5, 6, 7)
+TB = {1: 2, 2: 3, 4: 4, 6: 5, 8: 6, 10: 7}
 
 
 def tile_grappa_coil_group_rss_k6_kernel(
@@ -47,25 +56,44 @@ def tile_grappa_coil_group_rss_k6_kernel(
         wf_scales = keep.tile([P, 256], U8, name="wf_scales", align_bytes=64)
         gain = keep.tile([P, 4, 4], BF16, name="gain")
         warm = keep.tile([P, 1], F32, name="warm")
-        h_tmp = keep.tile([P, 4, PAIRS * 128], BF16, name="h_tmp", align_bytes=64)
-        h_fin = keep.tile([P, 2, 2, PAIRS * 128], BF16, name="h_fin", align_bytes=64)
-        h_codes = keep.tile([P, 2, 512], U32, name="h_codes", align_bytes=64)
-        h_scales = keep.tile([P, 2, 512], U8, name="h_scales", align_bytes=64)
+        h_codes = keep.tile([P, 2, 2, 2, 128], U32, name="h_codes", align_bytes=64)
+        h_scales = keep.tile([P, 2, 2, 2, 128], U8, name="h_scales", align_bytes=64)
+        h_bf, pre_codes, pre_scales = {}, {}, {}
+        for n in range(2):
+            h_bf[n] = keep.tile([P, 4, 512], BF16, name="h_bf%d" % n, align_bytes=64)
+            pre_codes[n] = keep.tile([P, 4, 128], U32, name="pre_codes%d" % n, align_bytes=64)
+            pre_scales[n] = keep.tile([P, 4, 128], U8, name="pre_scales%d" % n, align_bytes=64)
         y_scales = keep.tile([P, 2, 512], U8, name="y_scales", align_bytes=64)
 
         near_raw, far_raw, far_sorted, op_raw, rest_sb = {}, {}, {}, {}, {}
         grouped, codes, scales, acc, banks = {}, {}, {}, {}, {}
-        sq_re, sq_im, y_sb, y_bf, y_codes = {}, {}, {}, {}, {}
+        squares, sums, y_sb, y_bf, y_codes = {}, {}, {}, {}, {}
+
+        halves = (slice(0, 256), slice(256, 512))
+        units = [(i + d, n) for i in (0, 6) for n in range(2) for d in range(2)]
+        units = units[:4] + [(i, n) for i in range(2, 6) for n in range(2)] + units[4:]
 
         def bank(b):
             return psum.tile([P, 512], F32, name="bank%d" % b)
 
-        def load_pair(j):
-            near_raw[j] = ring.tile([P, 2, 1024], BF16, name="near_raw", bufs=LOADS_AHEAD)
-            nc.sync.dma_start(out=near_raw[j][:], in_=near_v[:, :, 1024 * j : 1024 * (j + 1)])
+        def load_near(j0, n):
+            raw = keep.tile([P, 2, 1024 * n], BF16, name="near%d" % j0)
+            nc.sync.dma_start(out=raw[:], in_=near_v[:, :, 1024 * j0 : 1024 * (j0 + n)])
+            words = raw[:].rearrange("p e x -> p (e x)").bitcast(F32)
+            for j in range(n):
+                for e in range(2):
+                    near_raw[j0 + j, e] = words[:, 512 * (n * e + j) : 512 * (n * e + j + 1)]
+
+        def load_far_half(e):
+            raw = keep.tile([P, 2048], BF16, name="far0%d" % e)
+            nc.sync.dma_start(out=raw[:], in_=far_v[:, e, 0:2048])
+            far_raw[0, e] = raw[:].bitcast(F32)
+
+        def load_far(j):
+            raw = ring.tile([P, 2, 2048], BF16, name="far_raw", bufs=FAR_BUFS)
+            nc.sync.dma_start(out=raw[:], in_=far_v[:, :, 2048 * j : 2048 * (j + 1)])
             for e in range(2):
-                far_raw[j, e] = ring.tile([P, 2048], BF16, name="far_raw", bufs=2 * LOADS_AHEAD)
-                nc.sync.dma_start(out=far_raw[j, e][:], in_=far_v[:, e, 2048 * j : 2048 * (j + 1)])
+                far_raw[j, e] = raw[:, e, :].bitcast(F32)
 
         def load_op(n):
             op_raw[n] = keep.tile([P, 2, 2048], BF16, name="op_raw%d" % n)
@@ -76,18 +104,20 @@ def tile_grappa_coil_group_rss_k6_kernel(
             nc.sync.dma_start(out=rest_sb[g][:], in_=rest_v[g])
 
         def sort_far(j, e):
+            if e not in SORTED:
+                return
             far_sorted[j, e] = ring.tile([P, 1024], F32, name="far_sorted", bufs=4)
             nc.vector.tensor_copy(
                 out=far_sorted[j, e][:].rearrange("p (s u j i) -> p s j u i", s=4, u=2, i=4),
-                in_=far_raw[j, e][:].bitcast(F32).rearrange("p (s j i u) -> p s j u i", s=4, u=2, i=4),
+                in_=far_raw[j, e].rearrange("p (s j i u) -> p s j u i", s=4, u=2, i=4),
             )
 
         def new_group(key):
             grouped[key] = ring.tile([P, 2048], BF16, name="grouped", bufs=4, align_bytes=64)
 
         def quantize(key):
-            codes[key] = ring.tile([P, 512], U32, name="codes", bufs=7, align_bytes=64)
-            scales[key] = ring.tile([P, 512], U8, name="scales", bufs=7, align_bytes=64)
+            codes[key] = ring.tile([P, 512], U32, name="codes", bufs=CODE_BUFS, align_bytes=64)
+            scales[key] = ring.tile([P, 512], U8, name="scales", bufs=CODE_BUFS, align_bytes=64)
             nc.vector.quantize_mx(out=codes[key][:].bitcast(FP8X4), scales=scales[key][:], in_=grouped[key][:])
 
         def turn_pair(j, q):
@@ -97,9 +127,10 @@ def tile_grappa_coil_group_rss_k6_kernel(
                 for h in range(2):
                     for u in range(2):
                         if q == 0:
-                            words = near_raw[j][:].rearrange("p e x -> p (e x)").bitcast(F32)
-                            base = 512 * s + 256 * h
-                            src = words[:, base + u : base + 256 : 2]
+                            src = near_raw[j, s][:, 256 * h + u : 256 * (h + 1) : 2]
+                        elif q - 1 not in SORTED:
+                            base = (2 * h + s) * 256
+                            src = far_raw[j, q - 1][:, base + u : base + 256 : 2]
                         else:
                             base = ((2 * h + s) * 2 + u) * 128
                             src = far_sorted[j, q - 1][:, base : base + 128]
@@ -141,29 +172,34 @@ def tile_grappa_coil_group_rss_k6_kernel(
 
         def gain_pair(j):
             nc.vector.tensor_tensor(
-                out=h_tmp[:, :, 128 * j : 128 * (j + 1)].rearrange("p r (c t) -> p r c t", t=4),
+                out=h_bf[j // 4][:, :, 128 * (j % 4) : 128 * (j % 4 + 1)].rearrange("p r (c t) -> p r c t", t=4),
                 in0=acc[j][:].rearrange("p (t r c) -> p r c t", t=4, r=4),
                 in1=gain[:].unsqueeze(2).to_broadcast([P, 4, 32, 4]),
                 op=ALU.mult,
             )
 
-        def swap(j0, j1):
-            cols = slice(128 * j0, 128 * j1)
-            for h in range(2):
-                for r in range(2):
-                    nc.sync.dma_start(
-                        out=h_fin[64 * r : 64 * (r + 1), :, h, cols],
-                        in_=h_tmp[64 * h : 64 * (h + 1), r::2, cols],
+        def quantize_h(n):
+            nc.vector.quantize_mx(
+                out=pre_codes[n][:].rearrange("p r c -> p (r c)").bitcast(FP8X4),
+                scales=pre_scales[n][:].rearrange("p r c -> p (r c)"),
+                in_=h_bf[n][:].rearrange("p r c -> p (r c)"),
+            )
+
+        def cross(n, queue):
+            for dst, src in ((h_codes, pre_codes[n]), (h_scales, pre_scales[n])):
+                for h in range(2):
+                    r = 1 - h
+                    queue.dma_start(
+                        out=dst[64 * r : 64 * (r + 1), :, n, h, :].bitcast(I32),
+                        in_=src[64 * h : 64 * (h + 1), r::2, :].bitcast(I32),
                     )
 
-        def quantize_h(j0, j1):
-            for g in range(2):
+        def stay(n):
+            for dst, src in ((h_codes, pre_codes[n]), (h_scales, pre_scales[n])):
                 for h in range(2):
-                    out_cols = slice(256 * h + 32 * j0, 256 * h + 32 * j1)
-                    nc.vector.quantize_mx(
-                        out=h_codes[:, g, out_cols].bitcast(FP8X4),
-                        scales=h_scales[:, g, out_cols],
-                        in_=h_fin[:, g, h, 128 * j0 : 128 * j1],
+                    nc.vector.tensor_copy(
+                        out=dst[64 * h : 64 * (h + 1), :, n, h, :].bitcast(I32),
+                        in_=src[64 * h : 64 * (h + 1), h::2, :].bitcast(I32),
                     )
 
         def turn_op(i):
@@ -189,41 +225,46 @@ def tile_grappa_coil_group_rss_k6_kernel(
             else:
                 nc.vector.tensor_copy(out=out, in_=src)
 
-        def multiply_op(i):
+        def multiply_unit(k):
+            i, n = units[k]
+            acc["unit", k] = bank(4 + k % 4)
             for a in range(2):
-                acc["op", i, a] = bank(4 + 2 * (i % 2) + a)
                 for g in range(2):
                     c0 = 256 * a + 128 * g
                     nc.tensor.matmul_mx(
-                        out=acc["op", i, a][:],
+                        out=acc["unit", k][:, 256 * a : 256 * (a + 1)],
                         lhsT=codes["op", i][:, c0 : c0 + 128].bitcast(FP8X4),
                         lhsT_scale=scales["op", i][:, c0 : c0 + 128],
-                        rhs=h_codes[:, g, :].bitcast(FP8X4),
-                        rhs_scale=h_scales[:, g, :],
+                        rhs=h_codes[:, g, n].rearrange("p h c -> p (h c)").bitcast(FP8X4),
+                        rhs_scale=h_scales[:, g, n].rearrange("p h c -> p (h c)"),
                         start=(g == 0),
                         stop=(g == 1),
                     )
 
-        def square(i):
-            sq_re[i] = ring.tile([P, 512], F32, name="sq_re", bufs=3)
-            sq_im[i] = ring.tile([P, 512], F32, name="sq_im", bufs=3)
-            for a, sq in enumerate((sq_re[i], sq_im[i])):
-                nc.scalar.activation(
-                    out=sq[:].rearrange("p (j h c) -> p j h c", h=2, c=32),
-                    in_=acc["op", i, a][:].rearrange("p (h j c) -> p j h c", h=2, c=32),
-                    func=ACT.Square,
-                )
+        def square(k):
+            squares[k] = ring.tile([P, 512], F32, name="squares", bufs=4)
+            nc.scalar.activation(out=squares[k][:], in_=acc["unit", k][:], func=ACT.Square)
 
-        def add_rest(i):
-            nc.vector.tensor_tensor(out=sq_re[i][:], in0=sq_re[i][:], in1=rest_sb[i // 4][:, i % 4, :], op=ALU.add)
+        def add_im(k):
+            sums[k] = ring.tile([P, 256], F32, name="sums", bufs=5)
+            nc.vector.tensor_tensor(out=sums[k][:], in0=squares[k][:, 0:256], in1=squares[k][:, 256:512], op=ALU.add)
 
-        def add_im(i, cols=slice(0, 512)):
-            nc.vector.tensor_tensor(out=sq_re[i][:, cols], in0=sq_re[i][:, cols], in1=sq_im[i][:, cols], op=ALU.add)
+        def add_rest(k):
+            i, n = units[k]
+            view = sums[k][:].rearrange("p (h j c) -> p j h c", h=2, c=32)
+            other = rest_sb[i // 4][:, i % 4, halves[n]].rearrange("p (j h c) -> p j h c", h=2, c=32)
+            nc.vector.tensor_tensor(out=view, in0=view, in1=other, op=ALU.add)
 
-        def root(i, cols=slice(0, 512)):
+        def root(k):
+            i, n = units[k]
             g, t = divmod(i, 4)
-            nc.scalar.activation(out=y_sb[g][:, t, cols], in_=sq_re[i][:, cols], func=ACT.Sqrt)
-            nc.sync.dma_start(out=y_v[g][:, t, cols], in_=y_sb[g][:, t, cols])
+            nc.scalar.activation(
+                out=y_sb[g][:, t, halves[n]].rearrange("p (j h c) -> p j h c", h=2, c=32),
+                in_=sums[k][:].rearrange("p (h j c) -> p j h c", h=2, c=32),
+                func=ACT.Sqrt,
+            )
+            if n == 1:
+                nc.sync.dma_start(out=y_v[g][:, t, :], in_=y_sb[g][:, t, :])
 
         def round_y(g, cols=slice(0, 512)):
             nc.vector.tensor_copy(
@@ -248,113 +289,119 @@ def tile_grappa_coil_group_rss_k6_kernel(
 
         nc.vector.memset(wf_scales[:].bitcast(I32), 0)
         nc.vector.memset(warm[:], 1.0)
+        for n in range(2):
+            nc.vector.memset(pre_scales[n][:].bitcast(I32), 0)
         make_identity(nc, ident[:])
-        for q in range(4):
-            nc.scalar.dma_start(
-                out=wf_scales[32 * q : 32 * q + 4, :].bitcast(I32).rearrange("p (g n) -> p g n", g=2),
-                in_=w_far_scales[:, 4 * q : 4 * q + 4, :].bitcast(I32).rearrange("g r n -> r g n"),
-            )
-        for h in range(2):
-            nc.scalar.dma_start(out=gain[64 * h : 64 * (h + 1)], in_=gain_v)
         nc.scalar.activation(out=warm[:], in_=warm[:], func=ACT.Sqrt)
-        load_pair(0)
+        load_near(0, 1)
+        load_far_half(0)
+        load_far_half(1)
         nc.sync.dma_start(out=wn_raw[:], in_=w_near.rearrange("(p j) n -> p j n", j=4))
         nc.sync.dma_start(
             out=wf_words[:].bitcast(I32).rearrange("p (g n) -> p g n", g=2),
             in_=w_far_words.bitcast(I32).rearrange("g p n -> p g n"),
         )
-        for j in range(1, LOADS_AHEAD):
-            load_pair(j)
+        load_near(1, 1)
+        load_far(1)
+        for q in range(4):
+            nc.sync.dma_start(
+                out=wf_scales[32 * q : 32 * q + 4, :].bitcast(I32).rearrange("p (g n) -> p g n", g=2),
+                in_=w_far_scales[:, 4 * q : 4 * q + 4, :].bitcast(I32).rearrange("g r n -> r g n"),
+            )
+        for h in range(2):
+            nc.sync.dma_start(out=gain[64 * h : 64 * (h + 1)], in_=gain_v)
+        for j in range(2, FAR_BUFS + 1):
+            if j % NEAR_N == 0:
+                load_near(j, NEAR_N)
+            load_far(j)
         sort_far(0, 0)
-        sort_far(0, 1)
-        nc.vector.tensor_copy(out=wn_grp[:], in_=wn_raw[:].rearrange("p j n -> p n j"))
 
         for j in range(PAIRS):
-            if j >= 2:
-                gain_pair(j - 2)
+            if j >= 1:
+                quantize((j - 1, 1))
+            sort_far(j, 1)
             if j >= 1:
                 quantize((j - 1, 2))
-            if j + 1 < PAIRS:
-                sort_far(j + 1, 0)
+            if j == 0:
+                nc.vector.tensor_copy(out=wn_grp[:], in_=wn_raw[:].rearrange("p j n -> p n j"))
+            if j >= 2:
+                gain_pair(j - 2)
+            for q in range(3):
+                turn_pair(j, q)
+            quantize((j, 0))
             if j == 0:
                 nc.vector.quantize_mx(
                     out=wn_codes[:].bitcast(FP8X4), scales=wn_scales[:], in_=wn_grp[:].rearrange("p n j -> p (n j)")
                 )
-            for q in range(3):
-                turn_pair(j, q)
-            quantize((j, 0))
             if j + 1 < PAIRS:
-                sort_far(j + 1, 1)
-            elif j + 1 == PAIRS:
-                quantize_h(0, 4)
-            quantize((j, 1))
-            if j >= 1:
-                multiply_pair(j - 1)
-            if j + LOADS_AHEAD < PAIRS:
-                load_pair(j + LOADS_AHEAD)
-            if j == 3:
-                load_op(0)
-            if j == 5:
-                swap(0, 4)
+                sort_far(j + 1, 0)
+            if j == QH:
+                quantize_h(0)
+                cross(0, nc.sync)
                 load_op(1)
                 load_rest(0)
+                load_op(2)
+                load_op(3)
+            if j >= 1:
+                multiply_pair(j - 1)
+            if j in (1, 2):
+                if (j + FAR_BUFS) % NEAR_N == 0:
+                    load_near(j + FAR_BUFS, NEAR_N)
+                load_far(j + FAR_BUFS)
+            if j == 3:
+                load_op(0)
 
+        stay(0)
+        quantize((PAIRS - 1, 1))
         gain_pair(PAIRS - 2)
         quantize((PAIRS - 1, 2))
         turn_op(0)
+        copy_op(0, 0, True)
+        copy_op(0, 1, True)
         multiply_pair(PAIRS - 1)
+        quantize(("op", 0))
         gain_pair(PAIRS - 1)
-        swap(4, 8)
-        load_op(2)
-        load_op(3)
+        turn_op(1)
+        copy_op(1, 0, True)
+        copy_op(1, 1, True)
+        quantize_h(1)
+        cross(1, nc.scalar)
         load_rest(1)
-        for i in range(4):
-            if i > 0:
-                turn_op(i)
-            copy_op(i, 0, True)
-            copy_op(i, 1, True)
-            if i < 3:
-                quantize(("op", i))
-        quantize_h(4, 8)
-        quantize(("op", 3))
+        quantize(("op", 1))
+        stay(1)
 
-        for i in range(0, TILES, 2):
-            ahead = i + 4 < TILES
-            multiply_op(i)
-            multiply_op(i + 1)
-            if ahead:
-                turn_op(i + 4)
-                turn_op(i + 5)
-            square(i)
-            if i == 6:
-                root(i - 1)
-            add_rest(i)
-            if i == 4:
-                round_y(0)
-            add_im(i)
-            square(i + 1)
-            add_rest(i + 1)
-            if i == 4:
+        turn_before = TB
+        UNITS = len(units)
+        for k in range(UNITS + 3):
+            n = turn_before.get(k)
+            if n is not None:
+                turn_op(n)
+            if k < UNITS:
+                multiply_unit(k)
+            if n is not None:
+                copy_op(n, 0, True)
+            if k < UNITS:
+                square(k)
+            if 1 <= k <= UNITS:
+                add_im(k - 1)
+            if n is not None:
+                copy_op(n, 1, n not in V_COPY)
+            if k - 1 in turn_before:
+                quantize(("op", turn_before[k - 1]))
+            if k in (R0, R0 + 1):
+                round_y(0, halves[k - R0])
+            if k == R0 + 2:
                 quantize_y(0)
-            if i + 2 < TILES:
-                add_im(i + 1)
-            root(i)
-            if ahead:
-                copy_op(i + 4, 0, True)
-                root(i + 1)
-                copy_op(i + 5, 0, True)
-                copy_op(i + 4, 1, False)
-                copy_op(i + 5, 1, False)
-                quantize(("op", i + 4))
-                quantize(("op", i + 5))
-        halves = (slice(0, 256), slice(256, 512))
-        for cols in halves:
-            add_im(TILES - 1, cols)
-            root(TILES - 1, cols)
-        for cols in halves:
-            round_y(1, cols)
-        for cols in halves:
-            quantize_y(1, cols)
+            if LA <= k < UNITS + LA:
+                add_rest(k - LA)
+            if k == UNITS + LR - 2:
+                round_y(1, halves[0])
+            if k == UNITS + LR - 1:
+                quantize_y(1, halves[0])
+            if LR <= k < UNITS + LR:
+                root(k - LR)
+        round_y(1, halves[1])
+        quantize_y(1, halves[1])
         for q in range(4):
             nc.scalar.dma_start(
                 out=out_2[:, 4 * q : 4 * q + 4, :].bitcast(I32).rearrange("g r m -> r g m"),

@@ -22,12 +22,13 @@ FAR_BUFS = 5
 SORTED = (0, 1)
 NEAR_N = 1
 CODE_BUFS = 7
-QH = 5
 LA = 2
 LR = 3
-R0 = 13
+R0 = (10, 12)
+Q0 = 13
+SQ_FIRST = False
 V_COPY = (2, 3, 4, 5, 6, 7)
-TB = {1: 2, 2: 3, 4: 4, 6: 5, 8: 6, 10: 7}
+TB = {1: (2,), 2: (3,), 4: (4,), 6: (5,), 8: (6,), 10: (7,)}
 
 
 def tile_grappa_coil_group_rss_k6_kernel(
@@ -48,6 +49,7 @@ def tile_grappa_coil_group_rss_k6_kernel(
         ctx.enter_context(tc.manual_schedule())
 
         ident = keep.tile([P, P], F32, name="ident")
+        perm = keep.tile([P, P], F32, name="perm")
         wn_raw = keep.tile([P, 4, 128], BF16, name="wn_raw")
         wn_grp = keep.tile([P, 128, 4], BF16, name="wn_grp", align_bytes=64)
         wn_codes = keep.tile([P, 128], U32, name="wn_codes", align_bytes=64)
@@ -134,12 +136,12 @@ def tile_grappa_coil_group_rss_k6_kernel(
                         else:
                             base = ((2 * h + s) * 2 + u) * 128
                             src = far_sorted[j, q - 1][:, base : base + 128]
-                        nc.tensor.transpose(bk[:, (2 * h + u) * 128 : (2 * h + u + 1) * 128], src, ident[:])
+                        nc.tensor.transpose(bk[:, (2 * h + u) * 128 : (2 * h + u + 1) * 128], src, perm[:])
                 nc.scalar.copy(
                     out=grouped[j, q][:, 1024 * s : 1024 * (s + 1)].bitcast(F32).rearrange(
                         "p (v h m u) -> p v h m u", v=2, h=2, u=2
                     ),
-                    in_=bk[:].rearrange("p (h u m v) -> p v h m u", h=2, u=2, v=2),
+                    in_=bk[:].rearrange("p (h u v m) -> p v h m u", h=2, u=2, v=2),
                 )
 
         def multiply_pair(j):
@@ -263,7 +265,9 @@ def tile_grappa_coil_group_rss_k6_kernel(
                 in_=sums[k][:].rearrange("p (h j c) -> p j h c", h=2, c=32),
                 func=ACT.Sqrt,
             )
-            if n == 1:
+            if i == TILES - 1:
+                nc.sync.dma_start(out=y_v[g][:, t, halves[n]], in_=y_sb[g][:, t, halves[n]])
+            elif n == 1:
                 nc.sync.dma_start(out=y_v[g][:, t, :], in_=y_sb[g][:, t, :])
 
         def round_y(g, cols=slice(0, 512)):
@@ -292,6 +296,9 @@ def tile_grappa_coil_group_rss_k6_kernel(
         for n in range(2):
             nc.vector.memset(pre_scales[n][:].bitcast(I32), 0)
         make_identity(nc, ident[:])
+        nc.vector.tensor_copy(
+            out=perm[:].rearrange("p (v m) -> p v m", v=2), in_=ident[:].rearrange("p (m v) -> p v m", v=2)
+        )
         nc.scalar.activation(out=warm[:], in_=warm[:], func=ACT.Sqrt)
         load_near(0, 1)
         load_far_half(0)
@@ -335,13 +342,10 @@ def tile_grappa_coil_group_rss_k6_kernel(
                 )
             if j + 1 < PAIRS:
                 sort_far(j + 1, 0)
-            if j == QH:
+            else:
                 quantize_h(0)
-                cross(0, nc.sync)
-                load_op(1)
-                load_rest(0)
+                cross(0, nc.scalar)
                 load_op(2)
-                load_op(3)
             if j >= 1:
                 multiply_pair(j - 1)
             if j in (1, 2):
@@ -350,11 +354,13 @@ def tile_grappa_coil_group_rss_k6_kernel(
                 load_far(j + FAR_BUFS)
             if j == 3:
                 load_op(0)
+                load_op(1)
+                load_rest(0)
 
-        stay(0)
         quantize((PAIRS - 1, 1))
         gain_pair(PAIRS - 2)
         quantize((PAIRS - 1, 2))
+        stay(0)
         turn_op(0)
         copy_op(0, 0, True)
         copy_op(0, 1, True)
@@ -366,44 +372,48 @@ def tile_grappa_coil_group_rss_k6_kernel(
         copy_op(1, 1, True)
         quantize_h(1)
         cross(1, nc.scalar)
+        load_op(3)
         load_rest(1)
         quantize(("op", 1))
         stay(1)
 
-        turn_before = TB
         UNITS = len(units)
-        for k in range(UNITS + 3):
-            n = turn_before.get(k)
-            if n is not None:
+        waiting = []
+        for k in range(UNITS + LR):
+            turned = TB.get(k, ())
+            for n in turned:
                 turn_op(n)
+            waiting.extend(turned)
             if k < UNITS:
                 multiply_unit(k)
-            if n is not None:
+            n = waiting.pop(0) if waiting else None
+            if n is not None and not SQ_FIRST:
                 copy_op(n, 0, True)
             if k < UNITS:
                 square(k)
+            if n is not None and SQ_FIRST:
+                copy_op(n, 0, True)
             if 1 <= k <= UNITS:
                 add_im(k - 1)
             if n is not None:
                 copy_op(n, 1, n not in V_COPY)
-            if k - 1 in turn_before:
-                quantize(("op", turn_before[k - 1]))
-            if k in (R0, R0 + 1):
-                round_y(0, halves[k - R0])
-            if k == R0 + 2:
-                quantize_y(0)
+            if k in R0:
+                round_y(0, halves[R0.index(k)])
             if LA <= k < UNITS + LA:
                 add_rest(k - LA)
+            if n is not None:
+                quantize(("op", n))
+            if k == Q0:
+                quantize_y(0)
             if k == UNITS + LR - 2:
                 round_y(1, halves[0])
-            if k == UNITS + LR - 1:
-                quantize_y(1, halves[0])
             if LR <= k < UNITS + LR:
                 root(k - LR)
         round_y(1, halves[1])
+        quantize_y(1, halves[0])
         quantize_y(1, halves[1])
         for q in range(4):
-            nc.scalar.dma_start(
+            (nc.scalar if q else nc.sync).dma_start(
                 out=out_2[:, 4 * q : 4 * q + 4, :].bitcast(I32).rearrange("g r m -> r g m"),
                 in_=y_scales[32 * q : 32 * q + 4].bitcast(I32),
             )

@@ -16,31 +16,42 @@ ALU = mybir.AluOpType
 FLOPS = 2 * 4096 * 1536 * 128 + 2 * 2048 * 1024 * 512
 
 P = 128
+HALF_P = 64
 PAIRS = 8
+PAIRS_PER_HALF = 4
 TILES = 8
+COLUMN_HALVES = (slice(0, 256), slice(256, 512))
+
 FAR_BUFS = 5
-SORTED = (0, 1)
-NEAR_N = 1
-CODE_BUFS = 7
-LA = 2
-LR = 3
-R0 = (10, 12)
-Q0 = 13
-SQ_FIRST = False
-V_COPY = (2, 3, 4, 5, 6, 7)
-TB = {1: (2,), 2: (3,), 4: (4,), 6: (5,), 8: (6,), 10: (7,)}
+SORTED_BUFS = 4
+GROUPED_BUFS = 4
+CODE_BUFS = 8
+SQUARE_BUFS = 4
+SUM_BUFS = 5
+
+EARLY_TILES = 4
+FIRST_HALF_STEP = PAIRS_PER_HALF + 1
+REST_LAG = 2
+ROOT_LAG = 3
+ROUND_STEPS = (8, 12)
+QUANTIZE_STEP = 13
 
 
 def tile_grappa_coil_group_rss_k6_kernel(
     tc, near, far, w_near, w_far_words, w_far_scales, line_gain, image_op, rest, out_0, out_1, out_2
 ):
     nc = tc.nc
-    near_v = near.rearrange("(p e f) k -> p e (f k)", p=P, e=2)
-    far_v = far.rearrange("(p e f) k -> p e (f k)", p=P, e=2)
-    op_v = image_op.rearrange("(a g p t) k -> g p a (t k)", a=2, g=2, t=4)
-    rest_v = rest.rearrange("(g p t) f c -> g p t (f c)", g=2, t=4)
-    y_v = out_0.rearrange("(g p t) f c -> g p t (f c)", g=2, t=4)
-    gain_v = line_gain.rearrange("(r q t) -> q r t", r=4, t=4)
+    near_rows = near.rearrange("(p e f) k -> p e (f k)", p=P, e=2)
+    far_rows = far.rearrange("(p e f) k -> p e (f k)", p=P, e=2)
+    op_rows = image_op.rearrange("(a g p t) k -> g p a (t k)", a=2, g=2, t=4)
+    rest_rows = rest.rearrange("(g p t) f c -> g p t (f c)", g=2, t=4)
+    y_rows = out_0.rearrange("(g p t) f c -> g p t (f c)", g=2, t=4)
+    gain_rows = line_gain.rearrange("(r am t) -> am r t", r=4, t=4)
+
+    units = [(i, n) for n in range(2) for i in range(EARLY_TILES)]
+    units += [(i, n) for i in range(EARLY_TILES, TILES - 2) for n in range(2)]
+    units += [(i, n) for n in range(2) for i in range(TILES - 2, TILES)]
+    turn_in_step = {max(i - 2, 2 * i - 5): i for i in range(2, TILES)}
 
     with ExitStack() as ctx:
         keep = ctx.enter_context(tc.tile_pool(name="keep", bufs=1))
@@ -51,13 +62,12 @@ def tile_grappa_coil_group_rss_k6_kernel(
         ident = keep.tile([P, P], F32, name="ident")
         perm = keep.tile([P, P], F32, name="perm")
         wn_raw = keep.tile([P, 4, 128], BF16, name="wn_raw")
-        wn_grp = keep.tile([P, 128, 4], BF16, name="wn_grp", align_bytes=64)
+        wn_grouped = keep.tile([P, 128, 4], BF16, name="wn_grouped", align_bytes=64)
         wn_codes = keep.tile([P, 128], U32, name="wn_codes", align_bytes=64)
         wn_scales = keep.tile([P, 128], U8, name="wn_scales", align_bytes=64)
         wf_words = keep.tile([P, 512], U8, name="wf_words", align_bytes=64)
         wf_scales = keep.tile([P, 256], U8, name="wf_scales", align_bytes=64)
         gain = keep.tile([P, 4, 4], BF16, name="gain")
-        warm = keep.tile([P, 1], F32, name="warm")
         h_codes = keep.tile([P, 2, 2, 2, 128], U32, name="h_codes", align_bytes=64)
         h_scales = keep.tile([P, 2, 2, 2, 128], U8, name="h_scales", align_bytes=64)
         h_bf, pre_codes, pre_scales = {}, {}, {}
@@ -67,105 +77,103 @@ def tile_grappa_coil_group_rss_k6_kernel(
             pre_scales[n] = keep.tile([P, 4, 128], U8, name="pre_scales%d" % n, align_bytes=64)
         y_scales = keep.tile([P, 2, 512], U8, name="y_scales", align_bytes=64)
 
-        near_raw, far_raw, far_sorted, op_raw, rest_sb = {}, {}, {}, {}, {}
-        grouped, codes, scales, acc, banks = {}, {}, {}, {}, {}
+        near_words, far_words, far_sorted, op_raw, rest_sb = {}, {}, {}, {}, {}
+        grouped, codes, scales = {}, {}, {}
+        pair_bank, op_bank, unit_bank = {}, {}, {}
         squares, sums, y_sb, y_bf, y_codes = {}, {}, {}, {}, {}
 
-        halves = (slice(0, 256), slice(256, 512))
-        units = [(i + d, n) for i in (0, 6) for n in range(2) for d in range(2)]
-        units = units[:4] + [(i, n) for i in range(2, 6) for n in range(2)] + units[4:]
+        def bank(index):
+            return psum.tile([P, 512], F32, name="bank%d" % index)
 
-        def bank(b):
-            return psum.tile([P, 512], F32, name="bank%d" % b)
-
-        def load_near(j0, n):
-            raw = keep.tile([P, 2, 1024 * n], BF16, name="near%d" % j0)
-            nc.sync.dma_start(out=raw[:], in_=near_v[:, :, 1024 * j0 : 1024 * (j0 + n)])
+        def load_near(j):
+            raw = keep.tile([P, 2, 1024], BF16, name="near%d" % j)
+            nc.sync.dma_start(out=raw[:], in_=near_rows[:, :, 1024 * j : 1024 * (j + 1)])
             words = raw[:].rearrange("p e x -> p (e x)").bitcast(F32)
-            for j in range(n):
-                for e in range(2):
-                    near_raw[j0 + j, e] = words[:, 512 * (n * e + j) : 512 * (n * e + j + 1)]
+            for e in range(2):
+                near_words[j, e] = words[:, 512 * e : 512 * (e + 1)]
 
-        def load_far_half(e):
-            raw = keep.tile([P, 2048], BF16, name="far0%d" % e)
-            nc.sync.dma_start(out=raw[:], in_=far_v[:, e, 0:2048])
-            far_raw[0, e] = raw[:].bitcast(F32)
+        def load_far_half(j, e):
+            raw = keep.tile([P, 2048], BF16, name="far_half%d" % e)
+            nc.sync.dma_start(out=raw[:], in_=far_rows[:, e, 2048 * j : 2048 * (j + 1)])
+            far_words[j, e] = raw[:].bitcast(F32)
 
         def load_far(j):
             raw = ring.tile([P, 2, 2048], BF16, name="far_raw", bufs=FAR_BUFS)
-            nc.sync.dma_start(out=raw[:], in_=far_v[:, :, 2048 * j : 2048 * (j + 1)])
+            nc.sync.dma_start(out=raw[:], in_=far_rows[:, :, 2048 * j : 2048 * (j + 1)])
             for e in range(2):
-                far_raw[j, e] = raw[:, e, :].bitcast(F32)
+                far_words[j, e] = raw[:, e, :].bitcast(F32)
 
-        def load_op(n):
-            op_raw[n] = keep.tile([P, 2, 2048], BF16, name="op_raw%d" % n)
-            nc.sync.dma_start(out=op_raw[n][:], in_=op_v[n // 2][:, :, 2048 * (n % 2) : 2048 * (n % 2 + 1)])
+        def load_far_scales(quadrant):
+            nc.sync.dma_start(
+                out=wf_scales[32 * quadrant : 32 * quadrant + 4, :].bitcast(I32).rearrange("p (g n) -> p g n", g=2),
+                in_=w_far_scales[:, 4 * quadrant : 4 * quadrant + 4, :].bitcast(I32).rearrange("g r n -> r g n"),
+            )
+
+        def load_op(load):
+            g, second = divmod(load, 2)
+            op_raw[load] = keep.tile([P, 2, 2048], BF16, name="op_raw%d" % load)
+            nc.sync.dma_start(out=op_raw[load][:], in_=op_rows[g][:, :, 2048 * second : 2048 * (second + 1)])
 
         def load_rest(g):
             rest_sb[g] = keep.tile([P, 4, 512], BF16, name="rest%d" % g)
-            nc.sync.dma_start(out=rest_sb[g][:], in_=rest_v[g])
+            nc.sync.dma_start(out=rest_sb[g][:], in_=rest_rows[g])
 
         def sort_far(j, e):
-            if e not in SORTED:
-                return
-            far_sorted[j, e] = ring.tile([P, 1024], F32, name="far_sorted", bufs=4)
+            far_sorted[j, e] = ring.tile([P, 1024], F32, name="far_sorted", bufs=SORTED_BUFS)
             nc.vector.tensor_copy(
-                out=far_sorted[j, e][:].rearrange("p (s u j i) -> p s j u i", s=4, u=2, i=4),
-                in_=far_raw[j, e].rearrange("p (s j i u) -> p s j u i", s=4, u=2, i=4),
+                out=far_sorted[j, e][:].rearrange("p (hg u x i) -> p hg x u i", hg=4, u=2, i=4),
+                in_=far_words[j, e].rearrange("p (hg x i u) -> p hg x u i", hg=4, u=2, i=4),
             )
 
         def new_group(key):
-            grouped[key] = ring.tile([P, 2048], BF16, name="grouped", bufs=4, align_bytes=64)
+            grouped[key] = ring.tile([P, 2048], BF16, name="grouped", bufs=GROUPED_BUFS, align_bytes=64)
 
         def quantize(key):
             codes[key] = ring.tile([P, 512], U32, name="codes", bufs=CODE_BUFS, align_bytes=64)
             scales[key] = ring.tile([P, 512], U8, name="scales", bufs=CODE_BUFS, align_bytes=64)
             nc.vector.quantize_mx(out=codes[key][:].bitcast(FP8X4), scales=scales[key][:], in_=grouped[key][:])
 
-        def turn_pair(j, q):
-            new_group((j, q))
-            for s in range(2):
-                bk = bank(2 * q + s)
+        def turn_pair(j, group):
+            new_group((j, group))
+            for side in range(2):
+                turned = bank(2 * group + side)
                 for h in range(2):
                     for u in range(2):
-                        if q == 0:
-                            src = near_raw[j, s][:, 256 * h + u : 256 * (h + 1) : 2]
-                        elif q - 1 not in SORTED:
-                            base = (2 * h + s) * 256
-                            src = far_raw[j, q - 1][:, base + u : base + 256 : 2]
+                        if group == 0:
+                            src = near_words[j, side][:, 256 * h + u : 256 * (h + 1) : 2]
                         else:
-                            base = ((2 * h + s) * 2 + u) * 128
-                            src = far_sorted[j, q - 1][:, base : base + 128]
-                        nc.tensor.transpose(bk[:, (2 * h + u) * 128 : (2 * h + u + 1) * 128], src, perm[:])
+                            start = ((2 * h + side) * 2 + u) * 128
+                            src = far_sorted[j, group - 1][:, start : start + 128]
+                        nc.tensor.transpose(turned[:, (2 * h + u) * 128 : (2 * h + u + 1) * 128], src, perm[:])
                 nc.scalar.copy(
-                    out=grouped[j, q][:, 1024 * s : 1024 * (s + 1)].bitcast(F32).rearrange(
-                        "p (v h m u) -> p v h m u", v=2, h=2, u=2
-                    ),
-                    in_=bk[:].rearrange("p (h u v m) -> p v h m u", h=2, u=2, v=2),
+                    out=grouped[j, group][:, 1024 * side : 1024 * (side + 1)]
+                    .bitcast(F32)
+                    .rearrange("p (v h am u) -> p v h am u", v=2, h=2, u=2),
+                    in_=turned[:].rearrange("p (h u v am) -> p v h am u", h=2, u=2, v=2),
                 )
 
         def multiply_pair(j):
-            acc[j] = bank(6 + j % 2)
+            pair_bank[j] = bank(6 + j % 2)
             for e in range(2):
                 for v in range(2):
                     t = 2 * v + e
-                    out = acc[j][:, 128 * t : 128 * (t + 1)]
-                    c0 = 256 * e + 128 * v
+                    out = pair_bank[j][:, 128 * t : 128 * (t + 1)]
+                    cols = slice(256 * e + 128 * v, 256 * e + 128 * (v + 1))
                     nc.tensor.matmul_mx(
                         out=out,
-                        lhsT=codes[j, 0][:, c0 : c0 + 128].bitcast(FP8X4),
-                        lhsT_scale=scales[j, 0][:, c0 : c0 + 128],
+                        lhsT=codes[j, 0][:, cols].bitcast(FP8X4),
+                        lhsT_scale=scales[j, 0][:, cols],
                         rhs=wn_codes[:].bitcast(FP8X4),
                         rhs_scale=wn_scales[:],
                         start=True,
                         stop=False,
                     )
                     for g in range(2):
-                        c0 = 256 * g + 128 * v
+                        cols = slice(256 * g + 128 * v, 256 * g + 128 * (v + 1))
                         nc.tensor.matmul_mx(
                             out=out,
-                            lhsT=codes[j, 1 + e][:, c0 : c0 + 128].bitcast(FP8X4),
-                            lhsT_scale=scales[j, 1 + e][:, c0 : c0 + 128],
+                            lhsT=codes[j, 1 + e][:, cols].bitcast(FP8X4),
+                            lhsT_scale=scales[j, 1 + e][:, cols],
                             rhs=wf_words[:, 256 * g : 256 * (g + 1)].bitcast(FP4X4),
                             rhs_scale=wf_scales[:, 128 * g : 128 * (g + 1)],
                             start=False,
@@ -173,9 +181,10 @@ def tile_grappa_coil_group_rss_k6_kernel(
                         )
 
         def gain_pair(j):
+            n, place = divmod(j, PAIRS_PER_HALF)
             nc.vector.tensor_tensor(
-                out=h_bf[j // 4][:, :, 128 * (j % 4) : 128 * (j % 4 + 1)].rearrange("p r (c t) -> p r c t", t=4),
-                in0=acc[j][:].rearrange("p (t r c) -> p r c t", t=4, r=4),
+                out=h_bf[n][:, :, 128 * place : 128 * (place + 1)].rearrange("p r (c t) -> p r c t", t=4),
+                in0=pair_bank[j][:].rearrange("p (t r c) -> p r c t", t=4, r=4),
                 in1=gain[:].unsqueeze(2).to_broadcast([P, 4, 32, 4]),
                 op=ALU.mult,
             )
@@ -187,103 +196,106 @@ def tile_grappa_coil_group_rss_k6_kernel(
                 in_=h_bf[n][:].rearrange("p r c -> p (r c)"),
             )
 
-        def cross(n, queue):
+        def cross(n):
             for dst, src in ((h_codes, pre_codes[n]), (h_scales, pre_scales[n])):
                 for h in range(2):
-                    r = 1 - h
-                    queue.dma_start(
-                        out=dst[64 * r : 64 * (r + 1), :, n, h, :].bitcast(I32),
-                        in_=src[64 * h : 64 * (h + 1), r::2, :].bitcast(I32),
+                    s = 1 - h
+                    nc.sync.dma_start(
+                        out=dst[HALF_P * s : HALF_P * (s + 1), :, n, h, :].bitcast(I32),
+                        in_=src[HALF_P * h : HALF_P * (h + 1), s::2, :].bitcast(I32),
                     )
 
         def stay(n):
             for dst, src in ((h_codes, pre_codes[n]), (h_scales, pre_scales[n])):
                 for h in range(2):
                     nc.vector.tensor_copy(
-                        out=dst[64 * h : 64 * (h + 1), :, n, h, :].bitcast(I32),
-                        in_=src[64 * h : 64 * (h + 1), h::2, :].bitcast(I32),
+                        out=dst[HALF_P * h : HALF_P * (h + 1), :, n, h, :].bitcast(I32),
+                        in_=src[HALF_P * h : HALF_P * (h + 1), h::2, :].bitcast(I32),
                     )
 
         def turn_op(i):
             new_group(("op", i))
             words = op_raw[i // 2][:].rearrange("p a x -> p (a x)").bitcast(F32)
             for a in range(2):
-                bk = bank(2 * (i % 2) + a)
-                banks[i, a] = bk
+                op_bank[i, a] = bank(2 * (i % 2) + a)
                 for g in range(2):
                     for u in range(2):
-                        base = 1024 * a + 512 * (i % 2) + 256 * g
+                        start = 1024 * a + 512 * (i % 2) + 256 * g
                         nc.tensor.transpose(
-                            bk[:, (2 * g + u) * 128 : (2 * g + u + 1) * 128],
-                            words[:, base + u : base + 256 : 2],
+                            op_bank[i, a][:, (2 * g + u) * 128 : (2 * g + u + 1) * 128],
+                            words[:, start + u : start + 256 : 2],
                             ident[:],
                         )
 
-        def copy_op(i, a, on_scalar):
-            out = grouped["op", i][:, 1024 * a : 1024 * (a + 1)].bitcast(F32).rearrange("p (g m u) -> p g m u", g=2, u=2)
-            src = banks[i, a][:].rearrange("p (g u m) -> p g m u", g=2, u=2)
-            if on_scalar:
-                nc.scalar.copy(out=out, in_=src)
-            else:
-                nc.vector.tensor_copy(out=out, in_=src)
+        def copy_op(i, a, copy):
+            copy(
+                out=grouped["op", i][:, 1024 * a : 1024 * (a + 1)]
+                .bitcast(F32)
+                .rearrange("p (g m u) -> p g m u", g=2, u=2),
+                in_=op_bank[i, a][:].rearrange("p (g u m) -> p g m u", g=2, u=2),
+            )
 
-        def multiply_unit(k):
-            i, n = units[k]
-            acc["unit", k] = bank(4 + k % 4)
+        def multiply_unit(step):
+            i, n = units[step]
+            unit_bank[step] = bank(4 + step % 4)
             for a in range(2):
                 for g in range(2):
-                    c0 = 256 * a + 128 * g
+                    cols = slice(256 * a + 128 * g, 256 * a + 128 * (g + 1))
                     nc.tensor.matmul_mx(
-                        out=acc["unit", k][:, 256 * a : 256 * (a + 1)],
-                        lhsT=codes["op", i][:, c0 : c0 + 128].bitcast(FP8X4),
-                        lhsT_scale=scales["op", i][:, c0 : c0 + 128],
+                        out=unit_bank[step][:, 256 * a : 256 * (a + 1)],
+                        lhsT=codes["op", i][:, cols].bitcast(FP8X4),
+                        lhsT_scale=scales["op", i][:, cols],
                         rhs=h_codes[:, g, n].rearrange("p h c -> p (h c)").bitcast(FP8X4),
                         rhs_scale=h_scales[:, g, n].rearrange("p h c -> p (h c)"),
                         start=(g == 0),
                         stop=(g == 1),
                     )
 
-        def square(k):
-            squares[k] = ring.tile([P, 512], F32, name="squares", bufs=4)
-            nc.scalar.activation(out=squares[k][:], in_=acc["unit", k][:], func=ACT.Square)
+        def square(step):
+            squares[step] = ring.tile([P, 512], F32, name="squares", bufs=SQUARE_BUFS)
+            nc.scalar.activation(out=squares[step][:], in_=unit_bank[step][:], func=ACT.Square)
 
-        def add_im(k):
-            sums[k] = ring.tile([P, 256], F32, name="sums", bufs=5)
-            nc.vector.tensor_tensor(out=sums[k][:], in0=squares[k][:, 0:256], in1=squares[k][:, 256:512], op=ALU.add)
+        def add_parts(step):
+            sums[step] = ring.tile([P, 256], F32, name="sums", bufs=SUM_BUFS)
+            nc.vector.tensor_tensor(
+                out=sums[step][:], in0=squares[step][:, 0:256], in1=squares[step][:, 256:512], op=ALU.add
+            )
 
-        def add_rest(k):
-            i, n = units[k]
-            view = sums[k][:].rearrange("p (h j c) -> p j h c", h=2, c=32)
-            other = rest_sb[i // 4][:, i % 4, halves[n]].rearrange("p (j h c) -> p j h c", h=2, c=32)
-            nc.vector.tensor_tensor(out=view, in0=view, in1=other, op=ALU.add)
+        def add_rest(step):
+            i, n = units[step]
+            total = sums[step][:].rearrange("p (h j c) -> p h j c", h=2, c=32)
+            other = rest_sb[i // 4][:, i % 4, COLUMN_HALVES[n]].rearrange("p (j h c) -> p h j c", h=2, c=32)
+            nc.vector.tensor_tensor(out=total, in0=total, in1=other, op=ALU.add)
 
-        def root(k):
-            i, n = units[k]
+        def root(step):
+            i, n = units[step]
             g, t = divmod(i, 4)
+            cols = COLUMN_HALVES[n]
             nc.scalar.activation(
-                out=y_sb[g][:, t, halves[n]].rearrange("p (j h c) -> p j h c", h=2, c=32),
-                in_=sums[k][:].rearrange("p (h j c) -> p j h c", h=2, c=32),
+                out=y_sb[g][:, t, cols].rearrange("p (j h c) -> p j h c", h=2, c=32),
+                in_=sums[step][:].rearrange("p (h j c) -> p j h c", h=2, c=32),
                 func=ACT.Sqrt,
             )
             if i == TILES - 1:
-                nc.sync.dma_start(out=y_v[g][:, t, halves[n]], in_=y_sb[g][:, t, halves[n]])
-            elif n == 1:
-                nc.sync.dma_start(out=y_v[g][:, t, :], in_=y_sb[g][:, t, :])
+                nc.sync.dma_start(out=y_rows[g][:, 2:4, cols], in_=y_sb[g][:, 2:4, cols])
+            elif n == 1 and i != TILES - 2:
+                nc.sync.dma_start(out=y_rows[g][:, t, :], in_=y_sb[g][:, t, :])
 
-        def round_y(g, cols=slice(0, 512)):
+        def round_y(g, cols):
             nc.vector.tensor_copy(
-                out=y_bf[g][:, cols, :].rearrange("p (c i) t -> p c t i", i=4),
-                in_=y_sb[g][:, :, cols].rearrange("p t (c i) -> p c t i", i=4),
+                out=y_bf[g][:, cols, :].rearrange("p (x i) t -> p x t i", i=4),
+                in_=y_sb[g][:, :, cols].rearrange("p t (x i) -> p x t i", i=4),
             )
 
-        def quantize_y(g, cols=slice(0, 512)):
+        def quantize_y(g, cols):
             nc.vector.quantize_mx(
                 out=y_codes[g][:, cols].bitcast(FP8X4),
                 scales=y_scales[:, g, cols],
                 in_=y_bf[g][:, cols, :].rearrange("p m t -> p (m t)"),
             )
             nc.sync.dma_start(
-                out=out_1[g][:, cols, :].rearrange("p m t -> p (m t)").bitcast(I32), in_=y_codes[g][:, cols].bitcast(I32)
+                out=out_1[g][:, cols, :].rearrange("p m t -> p (m t)").bitcast(I32),
+                in_=y_codes[g][:, cols].bitcast(I32),
             )
 
         for g in range(2):
@@ -292,128 +304,127 @@ def tile_grappa_coil_group_rss_k6_kernel(
             y_codes[g] = keep.tile([P, 512], U32, name="y_codes%d" % g, align_bytes=64)
 
         nc.vector.memset(wf_scales[:].bitcast(I32), 0)
-        nc.vector.memset(warm[:], 1.0)
         for n in range(2):
             nc.vector.memset(pre_scales[n][:].bitcast(I32), 0)
         make_identity(nc, ident[:])
-        nc.vector.tensor_copy(
-            out=perm[:].rearrange("p (v m) -> p v m", v=2), in_=ident[:].rearrange("p (m v) -> p v m", v=2)
+        nc.scalar.activation(
+            out=perm[:].rearrange("p (v am) -> p v am", v=2),
+            in_=ident[:].rearrange("p (am v) -> p v am", v=2),
+            func=ACT.Square,
         )
-        nc.scalar.activation(out=warm[:], in_=warm[:], func=ACT.Sqrt)
-        load_near(0, 1)
-        load_far_half(0)
-        load_far_half(1)
-        nc.sync.dma_start(out=wn_raw[:], in_=w_near.rearrange("(p j) n -> p j n", j=4))
+
+        load_near(0)
+        load_far_half(0, 0)
+        load_far_half(0, 1)
+        nc.sync.dma_start(out=wn_raw[:], in_=w_near.rearrange("(p t) n -> p t n", t=4))
         nc.sync.dma_start(
             out=wf_words[:].bitcast(I32).rearrange("p (g n) -> p g n", g=2),
             in_=w_far_words.bitcast(I32).rearrange("g p n -> p g n"),
         )
-        load_near(1, 1)
+        load_far_scales(0)
+        load_far_scales(1)
+        load_near(1)
         load_far(1)
-        for q in range(4):
-            nc.sync.dma_start(
-                out=wf_scales[32 * q : 32 * q + 4, :].bitcast(I32).rearrange("p (g n) -> p g n", g=2),
-                in_=w_far_scales[:, 4 * q : 4 * q + 4, :].bitcast(I32).rearrange("g r n -> r g n"),
-            )
+        load_far_scales(2)
+        load_far_scales(3)
+        load_near(2)
+        load_far(2)
         for h in range(2):
-            nc.sync.dma_start(out=gain[64 * h : 64 * (h + 1)], in_=gain_v)
-        for j in range(2, FAR_BUFS + 1):
-            if j % NEAR_N == 0:
-                load_near(j, NEAR_N)
+            nc.sync.dma_start(out=gain[HALF_P * h : HALF_P * (h + 1)], in_=gain_rows)
+        for j in range(3, FAR_BUFS + 1):
+            load_near(j)
             load_far(j)
         sort_far(0, 0)
 
+        last = PAIRS - 1
         for j in range(PAIRS):
             if j >= 1:
                 quantize((j - 1, 1))
             sort_far(j, 1)
             if j >= 1:
                 quantize((j - 1, 2))
-            if j == 0:
-                nc.vector.tensor_copy(out=wn_grp[:], in_=wn_raw[:].rearrange("p j n -> p n j"))
+            else:
+                nc.vector.tensor_copy(out=wn_grouped[:], in_=wn_raw[:].rearrange("p t n -> p n t"))
             if j >= 2:
                 gain_pair(j - 2)
-            for q in range(3):
-                turn_pair(j, q)
+            for group in range(3):
+                turn_pair(j, group)
             quantize((j, 0))
             if j == 0:
                 nc.vector.quantize_mx(
-                    out=wn_codes[:].bitcast(FP8X4), scales=wn_scales[:], in_=wn_grp[:].rearrange("p n j -> p (n j)")
+                    out=wn_codes[:].bitcast(FP8X4), scales=wn_scales[:], in_=wn_grouped[:].rearrange("p n t -> p (n t)")
                 )
-            if j + 1 < PAIRS:
+            if j < last:
                 sort_far(j + 1, 0)
-            else:
+            if j == FIRST_HALF_STEP:
                 quantize_h(0)
-                cross(0, nc.scalar)
+                cross(0)
+                load_op(1)
+                load_rest(0)
                 load_op(2)
             if j >= 1:
                 multiply_pair(j - 1)
-            if j in (1, 2):
-                if (j + FAR_BUFS) % NEAR_N == 0:
-                    load_near(j + FAR_BUFS, NEAR_N)
-                load_far(j + FAR_BUFS)
-            if j == 3:
+            if j == 1:
+                load_near(last - 1)
+                load_far(last - 1)
+                load_near(last)
+                load_far_half(last, 0)
+                load_far_half(last, 1)
                 load_op(0)
-                load_op(1)
-                load_rest(0)
 
-        quantize((PAIRS - 1, 1))
-        gain_pair(PAIRS - 2)
-        quantize((PAIRS - 1, 2))
-        stay(0)
+        quantize((last, 1))
+        quantize((last, 2))
+        gain_pair(last - 1)
         turn_op(0)
-        copy_op(0, 0, True)
-        copy_op(0, 1, True)
-        multiply_pair(PAIRS - 1)
+        copy_op(0, 0, nc.scalar.copy)
+        copy_op(0, 1, nc.scalar.copy)
+        multiply_pair(last)
+        stay(0)
+        gain_pair(last)
         quantize(("op", 0))
-        gain_pair(PAIRS - 1)
-        turn_op(1)
-        copy_op(1, 0, True)
-        copy_op(1, 1, True)
         quantize_h(1)
-        cross(1, nc.scalar)
+        turn_op(1)
+        copy_op(1, 0, nc.scalar.copy)
+        copy_op(1, 1, nc.scalar.copy)
+        cross(1)
         load_op(3)
         load_rest(1)
         quantize(("op", 1))
         stay(1)
 
-        UNITS = len(units)
-        waiting = []
-        for k in range(UNITS + LR):
-            turned = TB.get(k, ())
-            for n in turned:
-                turn_op(n)
-            waiting.extend(turned)
-            if k < UNITS:
-                multiply_unit(k)
-            n = waiting.pop(0) if waiting else None
-            if n is not None and not SQ_FIRST:
-                copy_op(n, 0, True)
-            if k < UNITS:
-                square(k)
-            if n is not None and SQ_FIRST:
-                copy_op(n, 0, True)
-            if 1 <= k <= UNITS:
-                add_im(k - 1)
-            if n is not None:
-                copy_op(n, 1, n not in V_COPY)
-            if k in R0:
-                round_y(0, halves[R0.index(k)])
-            if LA <= k < UNITS + LA:
-                add_rest(k - LA)
-            if n is not None:
-                quantize(("op", n))
-            if k == Q0:
-                quantize_y(0)
-            if k == UNITS + LR - 2:
-                round_y(1, halves[0])
-            if LR <= k < UNITS + LR:
-                root(k - LR)
-        round_y(1, halves[1])
-        quantize_y(1, halves[0])
-        quantize_y(1, halves[1])
-        for q in range(4):
-            (nc.scalar if q else nc.sync).dma_start(
-                out=out_2[:, 4 * q : 4 * q + 4, :].bitcast(I32).rearrange("g r m -> r g m"),
-                in_=y_scales[32 * q : 32 * q + 4].bitcast(I32),
+        count = len(units)
+        for step in range(count + ROOT_LAG):
+            i = turn_in_step.get(step)
+            if i is not None:
+                turn_op(i)
+            if step < count:
+                multiply_unit(step)
+            if i is not None:
+                copy_op(i, 0, nc.scalar.copy)
+            if step < count:
+                square(step)
+            if 1 <= step <= count:
+                add_parts(step - 1)
+            if i is not None:
+                copy_op(i, 1, nc.vector.tensor_copy)
+            if step in ROUND_STEPS:
+                round_y(0, COLUMN_HALVES[ROUND_STEPS.index(step)])
+            if REST_LAG <= step < count + REST_LAG:
+                add_rest(step - REST_LAG)
+            if i is not None:
+                quantize(("op", i))
+            if step == QUANTIZE_STEP:
+                quantize_y(0, slice(0, 512))
+            if step == count - 2 + ROOT_LAG:
+                round_y(1, COLUMN_HALVES[0])
+            if step >= ROOT_LAG:
+                root(step - ROOT_LAG)
+        round_y(1, COLUMN_HALVES[1])
+        for cols in COLUMN_HALVES:
+            quantize_y(1, cols)
+        for quadrant in range(4):
+            queue = nc.sync if quadrant == 0 else nc.scalar
+            queue.dma_start(
+                out=out_2[:, 4 * quadrant : 4 * quadrant + 4, :].bitcast(I32).rearrange("g r m -> r g m"),
+                in_=y_scales[32 * quadrant : 32 * quadrant + 4].bitcast(I32),
             )

@@ -60,7 +60,6 @@ def tile_grappa_coil_group_rss_k6_kernel(
         ctx.enter_context(tc.manual_schedule())
 
         ident = keep.tile([P, P], F32, name="ident")
-        perm = keep.tile([P, P], F32, name="perm")
         wn_raw = keep.tile([P, 4, 128], BF16, name="wn_raw")
         wn_grouped = keep.tile([P, 128, 4], BF16, name="wn_grouped", align_bytes=64)
         wn_codes = keep.tile([P, 128], U32, name="wn_codes", align_bytes=64)
@@ -68,6 +67,7 @@ def tile_grappa_coil_group_rss_k6_kernel(
         wf_words = keep.tile([P, 512], U8, name="wf_words", align_bytes=64)
         wf_scales = keep.tile([P, 256], U8, name="wf_scales", align_bytes=64)
         gain = keep.tile([P, 4, 4], BF16, name="gain")
+        warm = keep.tile([P, 1], F32, name="warm")
         h_codes = keep.tile([P, 2, 2, 2, 128], U32, name="h_codes", align_bytes=64)
         h_scales = keep.tile([P, 2, 2, 2, 128], U8, name="h_scales", align_bytes=64)
         h_bf, pre_codes, pre_scales = {}, {}, {}
@@ -144,12 +144,12 @@ def tile_grappa_coil_group_rss_k6_kernel(
                         else:
                             start = ((2 * h + side) * 2 + u) * 128
                             src = far_sorted[j, group - 1][:, start : start + 128]
-                        nc.tensor.transpose(turned[:, (2 * h + u) * 128 : (2 * h + u + 1) * 128], src, perm[:])
+                        nc.tensor.transpose(turned[:, (2 * h + u) * 128 : (2 * h + u + 1) * 128], src, ident[:])
                 nc.scalar.copy(
                     out=grouped[j, group][:, 1024 * side : 1024 * (side + 1)]
                     .bitcast(F32)
                     .rearrange("p (v h am u) -> p v h am u", v=2, h=2, u=2),
-                    in_=turned[:].rearrange("p (h u v am) -> p v h am u", h=2, u=2, v=2),
+                    in_=turned[:].rearrange("p (h u am v) -> p v h am u", h=2, u=2, v=2),
                 )
 
         def multiply_pair(j):
@@ -306,12 +306,9 @@ def tile_grappa_coil_group_rss_k6_kernel(
         nc.vector.memset(wf_scales[:].bitcast(I32), 0)
         for n in range(2):
             nc.vector.memset(pre_scales[n][:].bitcast(I32), 0)
+        nc.vector.memset(warm[:], 1.0)
         make_identity(nc, ident[:])
-        nc.scalar.activation(
-            out=perm[:].rearrange("p (v am) -> p v am", v=2),
-            in_=ident[:].rearrange("p (am v) -> p v am", v=2),
-            func=ACT.Square,
-        )
+        nc.scalar.activation(out=warm[:], in_=warm[:], func=ACT.Sqrt)
 
         load_near(0)
         load_far_half(0, 0)

from contextlib import ExitStack

import concourse.mybir as mybir
from concourse.masks import make_identity

F32 = mybir.dt.float32
BF16 = mybir.dt.bfloat16
I32 = mybir.dt.int32
U32 = mybir.dt.uint32
U8 = mybir.dt.uint8
FP8X4 = mybir.dt.float8_e4m3fn_x4
FP4X4 = mybir.dt.float4_e2m1fn_x4
ACT = mybir.ActivationFunctionType
ALU = mybir.AluOpType

FLOPS = 2 * 4096 * 1536 * 128 + 2 * 2048 * 1024 * 512

P = 128
HALF_P = 64
PAIRS = 8
PAIRS_PER_HALF = 4
TILES = 8
COLUMN_HALVES = (slice(0, 256), slice(256, 512))

FAR_BUFS = 5
SORTED_BUFS = 4
GROUPED_BUFS = 4
CODE_BUFS = 8
SQUARE_BUFS = 4
SUM_BUFS = 5

EARLY_TILES = 4
FIRST_HALF_STEP = PAIRS_PER_HALF + 1
REST_LAG = 2
ROOT_LAG = 3
ROUND_STEPS = (8, 12)
QUANTIZE_STEP = 13


def tile_grappa_coil_group_rss_k6_kernel(
    tc, near, far, w_near, w_far_words, w_far_scales, line_gain, image_op, rest, out_0, out_1, out_2
):
    nc = tc.nc
    near_rows = near.rearrange("(p e f) k -> p e (f k)", p=P, e=2)
    far_rows = far.rearrange("(p e f) k -> p e (f k)", p=P, e=2)
    op_rows = image_op.rearrange("(a g p t) k -> g p a (t k)", a=2, g=2, t=4)
    rest_rows = rest.rearrange("(g p t) f c -> g p t (f c)", g=2, t=4)
    y_rows = out_0.rearrange("(g p t) f c -> g p t (f c)", g=2, t=4)
    gain_rows = line_gain.rearrange("(r am t) -> am r t", r=4, t=4)

    units = [(i, n) for n in range(2) for i in range(EARLY_TILES)]
    units += [(i, n) for i in range(EARLY_TILES, TILES - 2) for n in range(2)]
    units += [(i, n) for n in range(2) for i in range(TILES - 2, TILES)]
    turn_in_step = {max(i - 2, 2 * i - 5): i for i in range(2, TILES)}

    with ExitStack() as ctx:
        keep = ctx.enter_context(tc.tile_pool(name="keep", bufs=1))
        ring = ctx.enter_context(tc.tile_pool(name="ring", bufs=1))
        psum = ctx.enter_context(tc.psum_pool(name="psum", bufs=1))
        ctx.enter_context(tc.manual_schedule())

        ident = keep.tile([P, P], F32, name="ident")
        wn_raw = keep.tile([P, 4, 128], BF16, name="wn_raw")
        wn_grouped = keep.tile([P, 128, 4], BF16, name="wn_grouped", align_bytes=64)
        wn_codes = keep.tile([P, 128], U32, name="wn_codes", align_bytes=64)
        wn_scales = keep.tile([P, 128], U8, name="wn_scales", align_bytes=64)
        wf_words = keep.tile([P, 512], U8, name="wf_words", align_bytes=64)
        wf_scales = keep.tile([P, 256], U8, name="wf_scales", align_bytes=64)
        gain = keep.tile([P, 4, 4], BF16, name="gain")
        warm = keep.tile([P, 1], F32, name="warm")
        h_codes = keep.tile([P, 2, 2, 2, 128], U32, name="h_codes", align_bytes=64)
        h_scales = keep.tile([P, 2, 2, 2, 128], U8, name="h_scales", align_bytes=64)
        h_bf, pre_codes, pre_scales = {}, {}, {}
        for n in range(2):
            h_bf[n] = keep.tile([P, 4, 512], BF16, name="h_bf%d" % n, align_bytes=64)
            pre_codes[n] = keep.tile([P, 4, 128], U32, name="pre_codes%d" % n, align_bytes=64)
            pre_scales[n] = keep.tile([P, 4, 128], U8, name="pre_scales%d" % n, align_bytes=64)
        y_scales = keep.tile([P, 2, 512], U8, name="y_scales", align_bytes=64)

        near_words, far_words, far_sorted, op_raw, rest_sb = {}, {}, {}, {}, {}
        grouped, codes, scales = {}, {}, {}
        pair_bank, op_bank, unit_bank = {}, {}, {}
        squares, sums, y_sb, y_bf, y_codes = {}, {}, {}, {}, {}

        def bank(index):
            return psum.tile([P, 512], F32, name="bank%d" % index)

        def load_near(j):
            raw = keep.tile([P, 2, 1024], BF16, name="near%d" % j)
            nc.sync.dma_start(out=raw[:], in_=near_rows[:, :, 1024 * j : 1024 * (j + 1)])
            words = raw[:].rearrange("p e x -> p (e x)").bitcast(F32)
            for e in range(2):
                near_words[j, e] = words[:, 512 * e : 512 * (e + 1)]

        def load_far_half(j, e):
            raw = keep.tile([P, 2048], BF16, name="far_half%d" % e)
            nc.sync.dma_start(out=raw[:], in_=far_rows[:, e, 2048 * j : 2048 * (j + 1)])
            far_words[j, e] = raw[:].bitcast(F32)

        def load_far(j):
            raw = ring.tile([P, 2, 2048], BF16, name="far_raw", bufs=FAR_BUFS)
            nc.sync.dma_start(out=raw[:], in_=far_rows[:, :, 2048 * j : 2048 * (j + 1)])
            for e in range(2):
                far_words[j, e] = raw[:, e, :].bitcast(F32)

        def load_far_scales(quadrant):
            nc.sync.dma_start(
                out=wf_scales[32 * quadrant : 32 * quadrant + 4, :].bitcast(I32).rearrange("p (g n) -> p g n", g=2),
                in_=w_far_scales[:, 4 * quadrant : 4 * quadrant + 4, :].bitcast(I32).rearrange("g r n -> r g n"),
            )

        def load_op(load):
            g, second = divmod(load, 2)
            op_raw[load] = keep.tile([P, 2, 2048], BF16, name="op_raw%d" % load)
            nc.sync.dma_start(out=op_raw[load][:], in_=op_rows[g][:, :, 2048 * second : 2048 * (second + 1)])

        def load_rest(g):
            rest_sb[g] = keep.tile([P, 4, 512], BF16, name="rest%d" % g)
            nc.sync.dma_start(out=rest_sb[g][:], in_=rest_rows[g])

        def sort_far(j, e):
            far_sorted[j, e] = ring.tile([P, 1024], F32, name="far_sorted", bufs=SORTED_BUFS)
            nc.vector.tensor_copy(
                out=far_sorted[j, e][:].rearrange("p (hg u x i) -> p hg x u i", hg=4, u=2, i=4),
                in_=far_words[j, e].rearrange("p (hg x i u) -> p hg x u i", hg=4, u=2, i=4),
            )

        def new_group(key):
            grouped[key] = ring.tile([P, 2048], BF16, name="grouped", bufs=GROUPED_BUFS, align_bytes=64)

        def quantize(key):
            codes[key] = ring.tile([P, 512], U32, name="codes", bufs=CODE_BUFS, align_bytes=64)
            scales[key] = ring.tile([P, 512], U8, name="scales", bufs=CODE_BUFS, align_bytes=64)
            nc.vector.quantize_mx(out=codes[key][:].bitcast(FP8X4), scales=scales[key][:], in_=grouped[key][:])

        def turn_pair(j, group):
            new_group((j, group))
            for side in range(2):
                turned = bank(2 * group + side)
                for h in range(2):
                    for u in range(2):
                        if group == 0:
                            src = near_words[j, side][:, 256 * h + u : 256 * (h + 1) : 2]
                        else:
                            start = ((2 * h + side) * 2 + u) * 128
                            src = far_sorted[j, group - 1][:, start : start + 128]
                        nc.tensor.transpose(turned[:, (2 * h + u) * 128 : (2 * h + u + 1) * 128], src, ident[:])
                nc.scalar.copy(
                    out=grouped[j, group][:, 1024 * side : 1024 * (side + 1)]
                    .bitcast(F32)
                    .rearrange("p (v h am u) -> p v h am u", v=2, h=2, u=2),
                    in_=turned[:].rearrange("p (h u am v) -> p v h am u", h=2, u=2, v=2),
                )

        def multiply_pair(j):
            pair_bank[j] = bank(6 + j % 2)
            for e in range(2):
                for v in range(2):
                    t = 2 * v + e
                    out = pair_bank[j][:, 128 * t : 128 * (t + 1)]
                    cols = slice(256 * e + 128 * v, 256 * e + 128 * (v + 1))
                    nc.tensor.matmul_mx(
                        out=out,
                        lhsT=codes[j, 0][:, cols].bitcast(FP8X4),
                        lhsT_scale=scales[j, 0][:, cols],
                        rhs=wn_codes[:].bitcast(FP8X4),
                        rhs_scale=wn_scales[:],
                        start=True,
                        stop=False,
                    )
                    for g in range(2):
                        cols = slice(256 * g + 128 * v, 256 * g + 128 * (v + 1))
                        nc.tensor.matmul_mx(
                            out=out,
                            lhsT=codes[j, 1 + e][:, cols].bitcast(FP8X4),
                            lhsT_scale=scales[j, 1 + e][:, cols],
                            rhs=wf_words[:, 256 * g : 256 * (g + 1)].bitcast(FP4X4),
                            rhs_scale=wf_scales[:, 128 * g : 128 * (g + 1)],
                            start=False,
                            stop=(g == 1),
                        )

        def gain_pair(j):
            n, place = divmod(j, PAIRS_PER_HALF)
            nc.vector.tensor_tensor(
                out=h_bf[n][:, :, 128 * place : 128 * (place + 1)].rearrange("p r (c t) -> p r c t", t=4),
                in0=pair_bank[j][:].rearrange("p (t r c) -> p r c t", t=4, r=4),
                in1=gain[:].unsqueeze(2).to_broadcast([P, 4, 32, 4]),
                op=ALU.mult,
            )

        def quantize_h(n):
            nc.vector.quantize_mx(
                out=pre_codes[n][:].rearrange("p r c -> p (r c)").bitcast(FP8X4),
                scales=pre_scales[n][:].rearrange("p r c -> p (r c)"),
                in_=h_bf[n][:].rearrange("p r c -> p (r c)"),
            )

        def cross(n):
            for dst, src in ((h_codes, pre_codes[n]), (h_scales, pre_scales[n])):
                for h in range(2):
                    s = 1 - h
                    nc.sync.dma_start(
                        out=dst[HALF_P * s : HALF_P * (s + 1), :, n, h, :].bitcast(I32),
                        in_=src[HALF_P * h : HALF_P * (h + 1), s::2, :].bitcast(I32),
                    )

        def stay(n):
            for dst, src in ((h_codes, pre_codes[n]), (h_scales, pre_scales[n])):
                for h in range(2):
                    nc.vector.tensor_copy(
                        out=dst[HALF_P * h : HALF_P * (h + 1), :, n, h, :].bitcast(I32),
                        in_=src[HALF_P * h : HALF_P * (h + 1), h::2, :].bitcast(I32),
                    )

        def turn_op(i):
            new_group(("op", i))
            words = op_raw[i // 2][:].rearrange("p a x -> p (a x)").bitcast(F32)
            for a in range(2):
                op_bank[i, a] = bank(2 * (i % 2) + a)
                for g in range(2):
                    for u in range(2):
                        start = 1024 * a + 512 * (i % 2) + 256 * g
                        nc.tensor.transpose(
                            op_bank[i, a][:, (2 * g + u) * 128 : (2 * g + u + 1) * 128],
                            words[:, start + u : start + 256 : 2],
                            ident[:],
                        )

        def copy_op(i, a, copy):
            copy(
                out=grouped["op", i][:, 1024 * a : 1024 * (a + 1)]
                .bitcast(F32)
                .rearrange("p (g m u) -> p g m u", g=2, u=2),
                in_=op_bank[i, a][:].rearrange("p (g u m) -> p g m u", g=2, u=2),
            )

        def multiply_unit(step):
            i, n = units[step]
            unit_bank[step] = bank(4 + step % 4)
            for a in range(2):
                for g in range(2):
                    cols = slice(256 * a + 128 * g, 256 * a + 128 * (g + 1))
                    nc.tensor.matmul_mx(
                        out=unit_bank[step][:, 256 * a : 256 * (a + 1)],
                        lhsT=codes["op", i][:, cols].bitcast(FP8X4),
                        lhsT_scale=scales["op", i][:, cols],
                        rhs=h_codes[:, g, n].rearrange("p h c -> p (h c)").bitcast(FP8X4),
                        rhs_scale=h_scales[:, g, n].rearrange("p h c -> p (h c)"),
                        start=(g == 0),
                        stop=(g == 1),
                    )

        def square(step):
            squares[step] = ring.tile([P, 512], F32, name="squares", bufs=SQUARE_BUFS)
            nc.scalar.activation(out=squares[step][:], in_=unit_bank[step][:], func=ACT.Square)

        def add_parts(step):
            sums[step] = ring.tile([P, 256], F32, name="sums", bufs=SUM_BUFS)
            nc.vector.tensor_tensor(
                out=sums[step][:], in0=squares[step][:, 0:256], in1=squares[step][:, 256:512], op=ALU.add
            )

        def add_rest(step):
            i, n = units[step]
            total = sums[step][:].rearrange("p (h j c) -> p h j c", h=2, c=32)
            other = rest_sb[i // 4][:, i % 4, COLUMN_HALVES[n]].rearrange("p (j h c) -> p h j c", h=2, c=32)
            nc.vector.tensor_tensor(out=total, in0=total, in1=other, op=ALU.add)

        def root(step):
            i, n = units[step]
            g, t = divmod(i, 4)
            cols = COLUMN_HALVES[n]
            nc.scalar.activation(
                out=y_sb[g][:, t, cols].rearrange("p (j h c) -> p j h c", h=2, c=32),
                in_=sums[step][:].rearrange("p (h j c) -> p j h c", h=2, c=32),
                func=ACT.Sqrt,
            )
            if i == TILES - 1:
                nc.sync.dma_start(out=y_rows[g][:, 2:4, cols], in_=y_sb[g][:, 2:4, cols])
            elif n == 1 and i != TILES - 2:
                nc.sync.dma_start(out=y_rows[g][:, t, :], in_=y_sb[g][:, t, :])

        def round_y(g, cols):
            nc.vector.tensor_copy(
                out=y_bf[g][:, cols, :].rearrange("p (x i) t -> p x t i", i=4),
                in_=y_sb[g][:, :, cols].rearrange("p t (x i) -> p x t i", i=4),
            )

        def quantize_y(g, cols):
            nc.vector.quantize_mx(
                out=y_codes[g][:, cols].bitcast(FP8X4),
                scales=y_scales[:, g, cols],
                in_=y_bf[g][:, cols, :].rearrange("p m t -> p (m t)"),
            )
            nc.sync.dma_start(
                out=out_1[g][:, cols, :].rearrange("p m t -> p (m t)").bitcast(I32),
                in_=y_codes[g][:, cols].bitcast(I32),
            )

        for g in range(2):
            y_sb[g] = keep.tile([P, 4, 512], F32, name="y%d" % g)
            y_bf[g] = keep.tile([P, 512, 4], BF16, name="y_bf%d" % g, align_bytes=64)
            y_codes[g] = keep.tile([P, 512], U32, name="y_codes%d" % g, align_bytes=64)

        nc.vector.memset(wf_scales[:].bitcast(I32), 0)
        for n in range(2):
            nc.vector.memset(pre_scales[n][:].bitcast(I32), 0)
        nc.vector.memset(warm[:], 1.0)
        make_identity(nc, ident[:])
        nc.scalar.activation(out=warm[:], in_=warm[:], func=ACT.Sqrt)

        load_near(0)
        load_far_half(0, 0)
        load_far_half(0, 1)
        nc.sync.dma_start(out=wn_raw[:], in_=w_near.rearrange("(p t) n -> p t n", t=4))
        nc.sync.dma_start(
            out=wf_words[:].bitcast(I32).rearrange("p (g n) -> p g n", g=2),
            in_=w_far_words.bitcast(I32).rearrange("g p n -> p g n"),
        )
        load_far_scales(0)
        load_far_scales(1)
        load_near(1)
        load_far(1)
        load_far_scales(2)
        load_far_scales(3)
        load_near(2)
        load_far(2)
        for h in range(2):
            nc.sync.dma_start(out=gain[HALF_P * h : HALF_P * (h + 1)], in_=gain_rows)
        for j in range(3, FAR_BUFS + 1):
            load_near(j)
            load_far(j)
        sort_far(0, 0)

        last = PAIRS - 1
        for j in range(PAIRS):
            if j >= 1:
                quantize((j - 1, 1))
            sort_far(j, 1)
            if j >= 1:
                quantize((j - 1, 2))
            else:
                nc.vector.tensor_copy(out=wn_grouped[:], in_=wn_raw[:].rearrange("p t n -> p n t"))
            if j >= 2:
                gain_pair(j - 2)
            for group in range(3):
                turn_pair(j, group)
            quantize((j, 0))
            if j == 0:
                nc.vector.quantize_mx(
                    out=wn_codes[:].bitcast(FP8X4), scales=wn_scales[:], in_=wn_grouped[:].rearrange("p n t -> p (n t)")
                )
            if j < last:
                sort_far(j + 1, 0)
            if j == FIRST_HALF_STEP:
                quantize_h(0)
                cross(0)
                load_op(1)
                load_rest(0)
                load_op(2)
            if j >= 1:
                multiply_pair(j - 1)
            if j == 1:
                load_near(last - 1)
                load_far(last - 1)
                load_near(last)
                load_far_half(last, 0)
                load_far_half(last, 1)
                load_op(0)

        quantize((last, 1))
        quantize((last, 2))
        gain_pair(last - 1)
        turn_op(0)
        copy_op(0, 0, nc.scalar.copy)
        copy_op(0, 1, nc.scalar.copy)
        multiply_pair(last)
        stay(0)
        gain_pair(last)
        quantize(("op", 0))
        quantize_h(1)
        turn_op(1)
        copy_op(1, 0, nc.scalar.copy)
        copy_op(1, 1, nc.scalar.copy)
        cross(1)
        load_op(3)
        load_rest(1)
        quantize(("op", 1))
        stay(1)

        count = len(units)
        for step in range(count + ROOT_LAG):
            i = turn_in_step.get(step)
            if i is not None:
                turn_op(i)
            if step < count:
                multiply_unit(step)
            if i is not None:
                copy_op(i, 0, nc.scalar.copy)
            if step < count:
                square(step)
            if 1 <= step <= count:
                add_parts(step - 1)
            if i is not None:
                copy_op(i, 1, nc.vector.tensor_copy)
            if step in ROUND_STEPS:
                round_y(0, COLUMN_HALVES[ROUND_STEPS.index(step)])
            if REST_LAG <= step < count + REST_LAG:
                add_rest(step - REST_LAG)
            if i is not None:
                quantize(("op", i))
            if step == QUANTIZE_STEP:
                quantize_y(0, slice(0, 512))
            if step == count - 2 + ROOT_LAG:
                round_y(1, COLUMN_HALVES[0])
            if step >= ROOT_LAG:
                root(step - ROOT_LAG)
        round_y(1, COLUMN_HALVES[1])
        for cols in COLUMN_HALVES:
            quantize_y(1, cols)
        for quadrant in range(4):
            queue = nc.sync if quadrant == 0 else nc.scalar
            queue.dma_start(
                out=out_2[:, 4 * quadrant : 4 * quadrant + 4, :].bitcast(I32).rearrange("g r m -> r g m"),
                in_=y_scales[32 * quadrant : 32 * quadrant + 4].bitcast(I32),
            )
